import numpy as np
import ml_dtypes


def mxq(x, axis, fmt="e4m3"):
    dtype, down = {"e4m3": (ml_dtypes.float8_e4m3fn, 7), "e5m2": (ml_dtypes.float8_e5m2, 14)}[fmt]
    v = np.moveaxis(np.asarray(x, np.float32).astype(ml_dtypes.bfloat16).astype(np.float64), axis, -1)
    blocks = v.reshape(v.shape[:-1] + (-1, 32))
    amax = np.abs(blocks).max(-1, keepdims=True)
    byte = np.maximum(np.where(amax > 0, np.frexp(amax)[1] - 1 + 127, 0) - down, 1)
    scale = np.exp2(byte - 127.0)
    codes = (blocks / scale).astype(np.float32).astype(dtype).astype(np.float64)
    return np.moveaxis((codes * scale).reshape(v.shape), -1, axis)


WIDE = False


def mx_kscale(k):
    if not WIDE:
        return np.ones(k)
    levels = np.array([10, -10, 5, -5, 0])
    if k % 512:
        return np.exp2(np.random.permutation(np.resize(levels, k // 32))).repeat(32)
    a = np.empty((k // 512, 16))
    for p in range(k // 512):
        a[p, :8] = np.random.permutation(np.resize(levels, 8))
        for g in range(8):
            far = levels[np.abs(levels - a[p, g]) >= 10]
            a[p, g + 8] = far[np.random.randint(len(far))]
    return np.exp2(a.ravel()).repeat(32)


def f64(x):
    return np.asarray(x).astype(np.float64)


def striped(idx):
    return np.tile(idx.reshape(-1, 16).T, (8, 1)).astype(np.uint16)


def unstriped(offs):
    return offs[:16].T.reshape(-1).astype(np.int64)


E2M1 = np.array([0.0, 0.5, 1.0, 1.5, 2.0, 3.0, 4.0, 6.0, -0.0, -0.5, -1.0, -1.5, -2.0, -3.0, -4.0, -6.0])


def pack_weight(w, fmt):
    k, n = w.shape
    w = f64(np.asarray(w, np.float32).astype(ml_dtypes.bfloat16)).reshape(k // 32, 32, n)
    amax = np.abs(w).max(1)
    if fmt == "e4m3":
        byte = np.frexp(amax)[1] - 1 + 127 - 7
    else:
        mant, ex = np.frexp(amax / 6.0)
        byte = np.where(mant > 0.5, ex, ex - 1) + 127
    byte = np.clip(np.where(amax > 0, byte, 1), 1, 254)
    scaled = (w * np.exp2(127.0 - byte)[:, None, :]).reshape(k, n).astype(np.float32)
    by_word = np.ascontiguousarray(scaled.reshape(k // 512, 128, 4, n).transpose(0, 1, 3, 2))
    if fmt == "e4m3":
        words = by_word.astype(ml_dtypes.float8_e4m3fn).view(np.uint8)
    else:
        c = by_word.astype(ml_dtypes.float4_e2m1fn).view(np.uint8) & 0xF
        words = (c[..., 0::2] | (c[..., 1::2] << 4)).reshape(k // 512, 128, 2 * n)
    return np.ascontiguousarray(words), np.ascontiguousarray(byte.astype(np.uint8).reshape(k // 512, 16, n))


def unpack_weight(words, scales, fmt):
    g, _, n = scales.shape
    words = np.ascontiguousarray(words).reshape(g, 128, n, -1)
    if fmt == "e4m3":
        vals = words.view(ml_dtypes.float8_e4m3fn).astype(np.float64)
    else:
        nib = np.empty((g, 128, n, 4), np.uint8)
        nib[..., 0::2] = words & 0xF
        nib[..., 1::2] = words >> 4
        vals = E2M1[nib]
    vals = vals * np.repeat(np.exp2(scales.astype(np.float64) - 127.0), 8, axis=1)[..., None]
    return vals.transpose(0, 1, 3, 2).reshape(g * 512, n)


K, T, E, G, H, N = 1024, 256, 8, 4, 512, 256


def setup_inputs():
    n = np.random.standard_normal
    s = mx_kscale(K)
    u = mx_kscale(H)
    chosen = np.random.permutation(E)[:G]
    x = pack_weight(n((K, T)) * s[:, None], "e4m3")
    w1 = pack_weight(n((K, E * H)) / np.sqrt(K) / s[:, None] * np.tile(u, E), "e4m3")
    w2 = pack_weight(n((H, E * N)) / np.sqrt(H) / u[:, None], "e4m3")
    return {
        "x_words": x[0],
        "x_scales": x[1],
        "w1_words": w1[0],
        "w1_scales": w1[1],
        "w2_words": w2[0],
        "w2_scales": w2[1],
        "gate": np.stack([np.tile(r, (128, 1)) for r in np.random.uniform(0.2, 1.0, (G, T))]).astype(np.float32),
        "offs": striped((chosen[:, None] * H + np.arange(H)).reshape(-1)),
        "offs2": striped((chosen[:, None] * N + np.arange(N)).reshape(-1)),
    }


def reference(x_words, x_scales, w1_words, w1_scales, w2_words, w2_scales, gate, offs, offs2):
    idx, idx2 = unstriped(offs), unstriped(offs2)
    x = unpack_weight(x_words, x_scales, "e4m3")
    w1 = unpack_weight(w1_words, w1_scales, "e4m3")[:, idx]
    w2 = unpack_weight(w2_words, w2_scales, "e4m3")[:, idx2]
    y = np.zeros((N, T))
    for r in range(G):
        h = f64(gate[r, :1]) * (w1[:, r * H:(r + 1) * H].T @ x)
        y = y + w2[:, r * N:(r + 1) * N].T @ mxq(h, 0, "e4m3")
    return y

@@ -1,0 +1,152 @@
+from contextlib import ExitStack
+
+import concourse.mybir as mybir
+from concourse.masks import make_identity
+
+K, T, E, G, H, N = 1024, 256, 8, 4, 512, 256
+FLOPS = 2 * G * T * H * (K + N)
+
+F32 = mybir.dt.float32
+BF16 = mybir.dt.bfloat16
+I32 = mybir.dt.int32
+U32 = mybir.dt.uint32
+U16 = mybir.dt.uint16
+U8 = mybir.dt.uint8
+FP8X4 = mybir.dt.float8_e4m3fn_x4
+COPY = mybir.ActivationFunctionType.Copy
+
+P = 128
+PASSES = K // 512
+QUADS = 4
+HALVES = T // P
+STAGE = P - 16
+
+
+def tile_moe_wsel_b_none_p_kernel(
+    tc, x_words, x_scales, w1_words, w1_scales, w2_words, w2_scales, gate, offs, offs2, out
+):
+    nc = tc.nc
+    with ExitStack() as ctx:
+        keep = ctx.enter_context(tc.tile_pool(name="keep", bufs=1))
+        work = ctx.enter_context(tc.tile_pool(name="work", bufs=2))
+        ps_h = ctx.enter_context(tc.psum_pool(name="ps_h", bufs=4))
+        ps_t = ctx.enter_context(tc.psum_pool(name="ps_t", bufs=2))
+        ps_o = ctx.enter_context(tc.psum_pool(name="ps_o", bufs=1))
+
+        list1 = keep.tile([P, G * H // 16], U16, name="list1")
+        list2 = keep.tile([P, G * N // 16], U16, name="list2")
+        w1s_all = keep.tile([P, E * H], U8, name="w1s_all", align_bytes=64)
+        w2s_all = keep.tile([P, E * N], U8, name="w2s_all", align_bytes=64)
+        w1w_all = [keep.tile([P, E * H], I32, name="w1w_all%d" % s, align_bytes=64) for s in range(PASSES)]
+        w2w_all = keep.tile([P, E * N], I32, name="w2w_all", align_bytes=64)
+        xw = keep.tile([P, PASSES, T], I32, name="xw", align_bytes=64)
+        xs = keep.tile([P, T], U8, name="xs", align_bytes=64)
+        w1s = keep.tile([P, G * H], U8, name="w1s", align_bytes=64)
+        w2s_picked = keep.tile([P, G * N], U8, name="w2s_picked", align_bytes=64)
+        w2s = keep.tile([P, G * N], U8, name="w2s", align_bytes=64)
+        gate_rows = keep.tile([P, P], F32, name="gate_rows")
+        gate_cols = keep.tile([P, G * HALVES], F32, name="gate_cols")
+        ident = keep.tile([P, P], F32, name="ident")
+
+        nc.vector.memset(w1s_all[:].bitcast(I32), 0)
+        nc.vector.memset(w2s_all[0:STAGE, :].bitcast(I32), 0)
+        nc.vector.memset(xs[:].bitcast(I32), 0)
+        nc.vector.memset(w2s[:].bitcast(I32), 0)
+        nc.gpsimd.memset(gate_rows[:], 0.0)
+        make_identity(nc, ident[:])
+
+        nc.sync.dma_start(list2[:], offs2)
+        nc.sync.dma_start(w2s_all[STAGE:P, :].bitcast(I32), w2_scales[0].bitcast(I32))
+        nc.sync.dma_start(list1[:], offs)
+        for q in range(QUADS):
+            nc.sync.dma_start(
+                w1s_all[32 * q : 32 * q + 4 * PASSES, :].bitcast(I32),
+                w1_scales[:, 4 * q : 4 * q + 4, :].bitcast(I32),
+            )
+        for s in range(PASSES):
+            nc.sync.dma_start(w1w_all[s][:], w1_words[s].rearrange("p m d -> p (m d)").bitcast(I32))
+        nc.sync.dma_start(xw[:], x_words.rearrange("s p t d -> p s (t d)").bitcast(I32))
+        nc.sync.dma_start(w2w_all[:], w2_words[0].rearrange("p m d -> p (m d)").bitcast(I32))
+        nc.scalar.dma_start(gate_rows[0 : G * HALVES, :], gate[:, 0, :].rearrange("r (h c) -> r h c", h=HALVES))
+        for q in range(QUADS):
+            nc.scalar.dma_start(
+                xs[32 * q : 32 * q + 4 * PASSES, :].bitcast(I32),
+                x_scales[:, 4 * q : 4 * q + 4, :].bitcast(I32),
+            )
+
+        gate_t = ps_t.tile([P, HALVES, 2, P], F32, name="turned")
+        nc.tensor.transpose(gate_t[:, 0, 0, :], gate_rows[:], ident[:])
+        nc.scalar.activation(gate_cols[:], gate_t[:, 0, 0, 0 : G * HALVES], COPY)
+
+        nc.vector.tensor_copy(w2s_picked[:], w2s_all[:].indirect(list2[:]))
+        for q in range(QUADS):
+            nc.sync.dma_start(
+                w2s[32 * q : 32 * q + 4, :].bitcast(I32),
+                w2s_picked[STAGE + 4 * q : STAGE + 4 * q + 4, :].bitcast(I32),
+            )
+        nc.vector.tensor_copy(w1s[:], w1s_all[:].indirect(list1[:]))
+
+        w1w = {}
+        for s in range(PASSES):
+            for r in range(G):
+                w1w[s, r] = keep.tile([P, H], I32, name="w1w_%d_%d" % (s, r), align_bytes=64)
+                nc.vector.tensor_copy(
+                    w1w[s, r][:].bitcast(U32),
+                    w1w_all[s][:].bitcast(U32).indirect(list1[:, r * H // 16 : (r + 1) * H // 16]),
+                )
+
+        acc = [ps_o.tile([P, T], F32, name="acc%d" % b) for b in range(N // P)]
+        for r in range(G):
+            turned = ps_t.tile([P, HALVES, 2, P], F32, name="turned")
+            for half in range(HALVES):
+                tok = slice(half * P, (half + 1) * P)
+                h_sum = ps_h.tile([P, H], F32, name="h_sum")
+                for s in range(PASSES):
+                    nc.tensor.matmul_mx(
+                        out=h_sum[:],
+                        lhsT=xw[:, s, tok].bitcast(FP8X4),
+                        lhsT_scale=xs[4 * s : P, tok],
+                        rhs=w1w[s, r][:].bitcast(FP8X4),
+                        rhs_scale=w1s[4 * s : P, r * H : (r + 1) * H],
+                        start=(s == 0),
+                        stop=(s == PASSES - 1),
+                    )
+                h_tok = work.tile([P, H], BF16, name="h_tok", bufs=4, align_bytes=64)
+                col = r * HALVES + half
+                nc.scalar.activation(
+                    h_tok[:].rearrange("t (u p e) -> t u p e", u=2, e=2),
+                    h_sum[:].rearrange("t (p u e) -> t u p e", u=2, e=2),
+                    COPY,
+                    scale=gate_cols[:, col : col + 1],
+                )
+                for u in range(2):
+                    nc.tensor.transpose(turned[:, half, u, :], h_tok[:].bitcast(F32)[:, u * P : (u + 1) * P], ident[:])
+            h_in = work.tile([P, 4 * T], BF16, name="h_in", bufs=4, align_bytes=64)
+            nc.scalar.copy(
+                h_in[:].bitcast(F32).rearrange("p (h t u) -> p h t u", h=HALVES, u=2),
+                turned[:].rearrange("p h u t -> p h t u"),
+            )
+            w2w = keep.tile([P, N], I32, name="w2w_%d" % r, align_bytes=64)
+            nc.vector.tensor_copy(
+                w2w[:].bitcast(U32),
+                w2w_all[:].bitcast(U32).indirect(list2[:, r * N // 16 : (r + 1) * N // 16]),
+            )
+            h_codes = work.tile([P, T], U32, name="h_codes", bufs=4, align_bytes=64)
+            h_scales = work.tile([P, T], U8, name="h_scales", bufs=4, align_bytes=64)
+            nc.vector.quantize_mx(out=h_codes[:].bitcast(FP8X4), scales=h_scales[:], in_=h_in[:])
+            for b in range(N // P):
+                nc.tensor.matmul_mx(
+                    out=acc[b][:],
+                    lhsT=w2w[:, b * P : (b + 1) * P].bitcast(FP8X4),
+                    lhsT_scale=w2s[:, r * N + b * P : r * N + (b + 1) * P],
+                    rhs=h_codes[:].bitcast(FP8X4),
+                    rhs_scale=h_scales[:],
+                    start=(r == 0),
+                    stop=(r == G - 1),
+                )
+
+        res = [keep.tile([P, T], F32, name="res%d" % b) for b in range(N // P)]
+        nc.scalar.copy(res[0][:], acc[0][:])
+        nc.sync.dma_start(out[0:P, :], res[0][:])
+        nc.vector.tensor_copy(res[1][:], acc[1][:])
+        nc.sync.dma_start(out[P : 2 * P, :], res[1][:])

@@ -29,9 +29,7 @@ def tile_moe_wsel_b_none_p_kernel(
     with ExitStack() as ctx:
         keep = ctx.enter_context(tc.tile_pool(name="keep", bufs=1))
         work = ctx.enter_context(tc.tile_pool(name="work", bufs=2))
-        ps_h = ctx.enter_context(tc.psum_pool(name="ps_h", bufs=4))
-        ps_t = ctx.enter_context(tc.psum_pool(name="ps_t", bufs=2))
-        ps_o = ctx.enter_context(tc.psum_pool(name="ps_o", bufs=1))
+        psum = ctx.enter_context(tc.psum_pool(name="psum", bufs=1))
 
         list1 = keep.tile([P, G * H // 16], U16, name="list1")
         list2 = keep.tile([P, G * N // 16], U16, name="list2")
@@ -48,35 +46,36 @@ def tile_moe_wsel_b_none_p_kernel(
         gate_cols = keep.tile([P, G * HALVES], F32, name="gate_cols")
         ident = keep.tile([P, P], F32, name="ident")
 
-        nc.vector.memset(w1s_all[:].bitcast(I32), 0)
-        nc.vector.memset(w2s_all[0:STAGE, :].bitcast(I32), 0)
-        nc.vector.memset(xs[:].bitcast(I32), 0)
-        nc.vector.memset(w2s[:].bitcast(I32), 0)
-        nc.gpsimd.memset(gate_rows[:], 0.0)
-        make_identity(nc, ident[:])
-
         nc.sync.dma_start(list2[:], offs2)
         nc.sync.dma_start(w2s_all[STAGE:P, :].bitcast(I32), w2_scales[0].bitcast(I32))
         nc.sync.dma_start(list1[:], offs)
+        nc.gpsimd.memset(w1s_all[:, 0 : E * H // 2].bitcast(I32), 0)
+        nc.vector.memset(w1s_all[:, E * H // 2 : E * H].bitcast(I32), 0)
+        nc.vector.memset(w2s_all[0:STAGE, :].bitcast(I32), 0)
+        make_identity(nc, ident[:])
+        nc.vector.memset(gate_rows[:], 0.0)
+        nc.vector.memset(xs[:].bitcast(I32), 0)
+        nc.vector.memset(w2s[:].bitcast(I32), 0)
+
         for q in range(QUADS):
             nc.sync.dma_start(
                 w1s_all[32 * q : 32 * q + 4 * PASSES, :].bitcast(I32),
                 w1_scales[:, 4 * q : 4 * q + 4, :].bitcast(I32),
             )
-        for s in range(PASSES):
-            nc.sync.dma_start(w1w_all[s][:], w1_words[s].rearrange("p m d -> p (m d)").bitcast(I32))
-        nc.sync.dma_start(xw[:], x_words.rearrange("s p t d -> p s (t d)").bitcast(I32))
-        nc.sync.dma_start(w2w_all[:], w2_words[0].rearrange("p m d -> p (m d)").bitcast(I32))
-        nc.scalar.dma_start(gate_rows[0 : G * HALVES, :], gate[:, 0, :].rearrange("r (h c) -> r h c", h=HALVES))
+        nc.sync.dma_start(w1w_all[0][:], w1_words[0].rearrange("p m d -> p (m d)").bitcast(I32))
+        nc.sync.dma_start(gate_rows[0 : G * HALVES, :], gate[:, 0, :].rearrange("r (h c) -> r h c", h=HALVES))
         for q in range(QUADS):
-            nc.scalar.dma_start(
+            nc.sync.dma_start(
                 xs[32 * q : 32 * q + 4 * PASSES, :].bitcast(I32),
                 x_scales[:, 4 * q : 4 * q + 4, :].bitcast(I32),
             )
+        nc.sync.dma_start(xw[:], x_words.rearrange("s p t d -> p s (t d)").bitcast(I32))
+        nc.sync.dma_start(w1w_all[1][:], w1_words[1].rearrange("p m d -> p (m d)").bitcast(I32))
+        nc.sync.dma_start(w2w_all[:], w2_words[0].rearrange("p m d -> p (m d)").bitcast(I32))
 
-        gate_t = ps_t.tile([P, HALVES, 2, P], F32, name="turned")
-        nc.tensor.transpose(gate_t[:, 0, 0, :], gate_rows[:], ident[:])
-        nc.scalar.activation(gate_cols[:], gate_t[:, 0, 0, 0 : G * HALVES], COPY)
+        gate_t = psum.tile([P, H], F32, name="gate_t", tag="bank%d" % (G * HALVES - 1))
+        nc.tensor.transpose(gate_t[:, 0:P], gate_rows[:], ident[:])
+        nc.scalar.activation(gate_cols[:], gate_t[:, 0 : G * HALVES], COPY)
 
         nc.vector.tensor_copy(w2s_picked[:], w2s_all[:].indirect(list2[:]))
         for q in range(QUADS):
@@ -95,12 +94,15 @@ def tile_moe_wsel_b_none_p_kernel(
                     w1w_all[s][:].bitcast(U32).indirect(list1[:, r * H // 16 : (r + 1) * H // 16]),
                 )
 
-        acc = [ps_o.tile([P, T], F32, name="acc%d" % b) for b in range(N // P)]
+        w2w = keep.tile([P, G * N], I32, name="w2w", align_bytes=64)
+        nc.vector.tensor_copy(w2w[:].bitcast(U32), w2w_all[:].bitcast(U32).indirect(list2[:]))
+
+        turned = []
         for r in range(G):
-            turned = ps_t.tile([P, HALVES, 2, P], F32, name="turned")
             for half in range(HALVES):
                 tok = slice(half * P, (half + 1) * P)
-                h_sum = ps_h.tile([P, H], F32, name="h_sum")
+                col = r * HALVES + half
+                h_sum = psum.tile([P, H], F32, name="h_sum", tag="bank%d" % col)
                 for s in range(PASSES):
                     nc.tensor.matmul_mx(
                         out=h_sum[:],
@@ -111,8 +113,9 @@ def tile_moe_wsel_b_none_p_kernel(
                         start=(s == 0),
                         stop=(s == PASSES - 1),
                     )
+                if half == 0:
+                    turned.append(h_sum[:].rearrange("p (h u t) -> p h u t", h=HALVES, u=2))
                 h_tok = work.tile([P, H], BF16, name="h_tok", bufs=4, align_bytes=64)
-                col = r * HALVES + half
                 nc.scalar.activation(
                     h_tok[:].rearrange("t (u p e) -> t u p e", u=2, e=2),
                     h_sum[:].rearrange("t (p u e) -> t u p e", u=2, e=2),
@@ -120,25 +123,24 @@ def tile_moe_wsel_b_none_p_kernel(
                     scale=gate_cols[:, col : col + 1],
                 )
                 for u in range(2):
-                    nc.tensor.transpose(turned[:, half, u, :], h_tok[:].bitcast(F32)[:, u * P : (u + 1) * P], ident[:])
+                    nc.tensor.transpose(turned[r][:, half, u, :], h_tok[:].bitcast(F32)[:, u * P : (u + 1) * P], ident[:])
+
+        acc = [psum.tile([P, H], F32, name="acc%d" % b, tag="bank%d" % (2 * b + 1)) for b in range(N // P)]
+        for r in range(G):
             h_in = work.tile([P, 4 * T], BF16, name="h_in", bufs=4, align_bytes=64)
             nc.scalar.copy(
                 h_in[:].bitcast(F32).rearrange("p (h t u) -> p h t u", h=HALVES, u=2),
-                turned[:].rearrange("p h u t -> p h t u"),
-            )
-            w2w = keep.tile([P, N], I32, name="w2w_%d" % r, align_bytes=64)
-            nc.vector.tensor_copy(
-                w2w[:].bitcast(U32),
-                w2w_all[:].bitcast(U32).indirect(list2[:, r * N // 16 : (r + 1) * N // 16]),
+                turned[r].rearrange("p h u t -> p h t u"),
             )
             h_codes = work.tile([P, T], U32, name="h_codes", bufs=4, align_bytes=64)
             h_scales = work.tile([P, T], U8, name="h_scales", bufs=4, align_bytes=64)
             nc.vector.quantize_mx(out=h_codes[:].bitcast(FP8X4), scales=h_scales[:], in_=h_in[:])
             for b in range(N // P):
+                cols = slice(r * N + b * P, r * N + (b + 1) * P)
                 nc.tensor.matmul_mx(
-                    out=acc[b][:],
-                    lhsT=w2w[:, b * P : (b + 1) * P].bitcast(FP8X4),
-                    lhsT_scale=w2s[:, r * N + b * P : r * N + (b + 1) * P],
+                    out=acc[b][:, 0:T],
+                    lhsT=w2w[:, cols].bitcast(FP8X4),
+                    lhsT_scale=w2s[:, cols],
                     rhs=h_codes[:].bitcast(FP8X4),
                     rhs_scale=h_scales[:],
                     start=(r == 0),
@@ -146,7 +148,7 @@ def tile_moe_wsel_b_none_p_kernel(
                 )
 
         res = [keep.tile([P, T], F32, name="res%d" % b) for b in range(N // P)]
-        nc.scalar.copy(res[0][:], acc[0][:])
-        nc.sync.dma_start(out[0:P, :], res[0][:])
-        nc.vector.tensor_copy(res[1][:], acc[1][:])
+        nc.scalar.copy(res[0][:], acc[0][:, 0:T])
+        nc.scalar.dma_start(out[0:P, :], res[0][:])
+        nc.vector.tensor_copy(res[1][:], acc[1][:, 0:T])
         nc.sync.dma_start(out[P : 2 * P, :], res[1][:])

@@ -19,7 +19,7 @@ P = 128
 PASSES = K // 512
 QUADS = 4
 HALVES = T // P
-STAGE = P - 16
+STAGE = P - 16 * PASSES
 
 
 def tile_moe_wsel_b_none_p_kernel(
@@ -39,29 +39,22 @@ def tile_moe_wsel_b_none_p_kernel(
         w2w_all = keep.tile([P, E * N], I32, name="w2w_all", align_bytes=64)
         xw = keep.tile([P, PASSES, T], I32, name="xw", align_bytes=64)
         xs = keep.tile([P, T], U8, name="xs", align_bytes=64)
+        w1s_picked = keep.tile([P, G * H], U8, name="w1s_picked", align_bytes=64)
         w1s = keep.tile([P, G * H], U8, name="w1s", align_bytes=64)
-        w2s_picked = keep.tile([P, G * N], U8, name="w2s_picked", align_bytes=64)
         w2s = keep.tile([P, G * N], U8, name="w2s", align_bytes=64)
         gate_rows = keep.tile([P, P], F32, name="gate_rows")
         gate_cols = keep.tile([P, G * HALVES], F32, name="gate_cols")
         ident = keep.tile([P, P], F32, name="ident")
 
-        nc.sync.dma_start(list2[:], offs2)
-        nc.sync.dma_start(w2s_all[STAGE:P, :].bitcast(I32), w2_scales[0].bitcast(I32))
-        nc.sync.dma_start(list1[:], offs)
-        nc.gpsimd.memset(w1s_all[:, 0 : E * H // 2].bitcast(I32), 0)
-        nc.vector.memset(w1s_all[:, E * H // 2 : E * H].bitcast(I32), 0)
-        nc.vector.memset(w2s_all[0:STAGE, :].bitcast(I32), 0)
-        make_identity(nc, ident[:])
-        nc.vector.memset(gate_rows[:], 0.0)
+        nc.vector.memset(w1s_all[0:STAGE, :].bitcast(I32), 0)
         nc.vector.memset(xs[:].bitcast(I32), 0)
-        nc.vector.memset(w2s[:].bitcast(I32), 0)
+        nc.vector.memset(w1s[:].bitcast(I32), 0)
+        nc.gpsimd.memset(gate_rows[:], 0.0)
+        make_identity(nc, ident[:])
+        nc.gpsimd.memset(w2s_all[:].bitcast(I32), 0)
 
-        for q in range(QUADS):
-            nc.sync.dma_start(
-                w1s_all[32 * q : 32 * q + 4 * PASSES, :].bitcast(I32),
-                w1_scales[:, 4 * q : 4 * q + 4, :].bitcast(I32),
-            )
+        nc.sync.dma_start(w1s_all[STAGE:P, :].bitcast(I32), w1_scales.rearrange("s b m -> (s b) m").bitcast(I32))
+        nc.sync.dma_start(list1[:], offs)
         nc.sync.dma_start(w1w_all[0][:], w1_words[0].rearrange("p m d -> p (m d)").bitcast(I32))
         nc.sync.dma_start(gate_rows[0 : G * HALVES, :], gate[:, 0, :].rearrange("r (h c) -> r h c", h=HALVES))
         for q in range(QUADS):
@@ -71,33 +64,40 @@ def tile_moe_wsel_b_none_p_kernel(
             )
         nc.sync.dma_start(xw[:], x_words.rearrange("s p t d -> p s (t d)").bitcast(I32))
         nc.sync.dma_start(w1w_all[1][:], w1_words[1].rearrange("p m d -> p (m d)").bitcast(I32))
+
+        nc.vector.tensor_copy(w1s_picked[:], w1s_all[:].indirect(list1[:]))
+        for s in range(PASSES):
+            for j in range(4):
+                first = STAGE + 16 * s + j
+                queue = nc.gpsimd if (s, j) == (PASSES - 1, 3) else nc.sync
+                queue.dma_start(
+                    w1s[4 * s + j : P : 32, :].bitcast(I32),
+                    w1s_picked[first : first + 13 : 4, :].bitcast(I32),
+                )
+        nc.sync.dma_start(list2[:], offs2)
+        for j in range(4):
+            nc.sync.dma_start(w2s_all[j:P:32, :].bitcast(I32), w2_scales[0, j:16:4, :].bitcast(I32))
         nc.sync.dma_start(w2w_all[:], w2_words[0].rearrange("p m d -> p (m d)").bitcast(I32))
 
         gate_t = psum.tile([P, H], F32, name="gate_t", tag="bank%d" % (G * HALVES - 1))
         nc.tensor.transpose(gate_t[:, 0:P], gate_rows[:], ident[:])
         nc.scalar.activation(gate_cols[:], gate_t[:, 0 : G * HALVES], COPY)
 
-        nc.vector.tensor_copy(w2s_picked[:], w2s_all[:].indirect(list2[:]))
-        for q in range(QUADS):
-            nc.sync.dma_start(
-                w2s[32 * q : 32 * q + 4, :].bitcast(I32),
-                w2s_picked[STAGE + 4 * q : STAGE + 4 * q + 4, :].bitcast(I32),
-            )
-        nc.vector.tensor_copy(w1s[:], w1s_all[:].indirect(list1[:]))
-
+        w1w_first = keep.tile([P, G * H], I32, name="w1w_first", align_bytes=64)
+        nc.vector.tensor_copy(w1w_first[:].bitcast(U32), w1w_all[0][:].bitcast(U32).indirect(list1[:]))
         w1w = {}
-        for s in range(PASSES):
-            for r in range(G):
-                w1w[s, r] = keep.tile([P, H], I32, name="w1w_%d_%d" % (s, r), align_bytes=64)
-                nc.vector.tensor_copy(
-                    w1w[s, r][:].bitcast(U32),
-                    w1w_all[s][:].bitcast(U32).indirect(list1[:, r * H // 16 : (r + 1) * H // 16]),
-                )
-
-        w2w = keep.tile([P, G * N], I32, name="w2w", align_bytes=64)
-        nc.vector.tensor_copy(w2w[:].bitcast(U32), w2w_all[:].bitcast(U32).indirect(list2[:]))
+        for r in range(G):
+            w1w[0, r] = w1w_first[:, r * H : (r + 1) * H]
+            second = keep.tile([P, H], I32, name="w1w_second%d" % r, align_bytes=64)
+            nc.vector.tensor_copy(
+                second[:].bitcast(U32),
+                w1w_all[1][:].bitcast(U32).indirect(list1[:, r * H // 16 : (r + 1) * H // 16]),
+            )
+            w1w[1, r] = second[:]
+        nc.vector.tensor_copy(w2s[:], w2s_all[:].indirect(list2[:]))
 
         turned = []
+        h_toks = []
         for r in range(G):
             for half in range(HALVES):
                 tok = slice(half * P, (half + 1) * P)
@@ -108,22 +108,26 @@ def tile_moe_wsel_b_none_p_kernel(
                         out=h_sum[:],
                         lhsT=xw[:, s, tok].bitcast(FP8X4),
                         lhsT_scale=xs[4 * s : P, tok],
-                        rhs=w1w[s, r][:].bitcast(FP8X4),
+                        rhs=w1w[s, r].bitcast(FP8X4),
                         rhs_scale=w1s[4 * s : P, r * H : (r + 1) * H],
                         start=(s == 0),
                         stop=(s == PASSES - 1),
                     )
                 if half == 0:
                     turned.append(h_sum[:].rearrange("p (h u t) -> p h u t", h=HALVES, u=2))
-                h_tok = work.tile([P, H], BF16, name="h_tok", bufs=4, align_bytes=64)
+                h_tok = work.tile([P, H], BF16, name="h_tok", bufs=G * HALVES, align_bytes=64)
                 nc.scalar.activation(
                     h_tok[:].rearrange("t (u p e) -> t u p e", u=2, e=2),
                     h_sum[:].rearrange("t (p u e) -> t u p e", u=2, e=2),
                     COPY,
                     scale=gate_cols[:, col : col + 1],
                 )
+                h_toks.append(h_tok)
+        for r in range(G):
+            for half in range(HALVES):
+                words = h_toks[r * HALVES + half][:].bitcast(F32)
                 for u in range(2):
-                    nc.tensor.transpose(turned[r][:, half, u, :], h_tok[:].bitcast(F32)[:, u * P : (u + 1) * P], ident[:])
+                    nc.tensor.transpose(turned[r][:, half, u, :], words[:, u * P : (u + 1) * P], ident[:])
 
         acc = [psum.tile([P, H], F32, name="acc%d" % b, tag="bank%d" % (2 * b + 1)) for b in range(N // P)]
         for r in range(G):
@@ -132,6 +136,11 @@ def tile_moe_wsel_b_none_p_kernel(
                 h_in[:].bitcast(F32).rearrange("p (h t u) -> p h t u", h=HALVES, u=2),
                 turned[r].rearrange("p h u t -> p h t u"),
             )
+            w2w = keep.tile([P, N], I32, name="w2w_%d" % r, align_bytes=64)
+            nc.vector.tensor_copy(
+                w2w[:].bitcast(U32),
+                w2w_all[:].bitcast(U32).indirect(list2[:, r * N // 16 : (r + 1) * N // 16]),
+            )
             h_codes = work.tile([P, T], U32, name="h_codes", bufs=4, align_bytes=64)
             h_scales = work.tile([P, T], U8, name="h_scales", bufs=4, align_bytes=64)
             nc.vector.quantize_mx(out=h_codes[:].bitcast(FP8X4), scales=h_scales[:], in_=h_in[:])
@@ -139,7 +148,7 @@ def tile_moe_wsel_b_none_p_kernel(
                 cols = slice(r * N + b * P, r * N + (b + 1) * P)
                 nc.tensor.matmul_mx(
                     out=acc[b][:, 0:T],
-                    lhsT=w2w[:, cols].bitcast(FP8X4),
+                    lhsT=w2w[:, b * P : (b + 1) * P].bitcast(FP8X4),
                     lhsT_scale=w2s[:, cols],
                     rhs=h_codes[:].bitcast(FP8X4),
                     rhs_scale=h_scales[:],

@@ -85,76 +85,96 @@ def tile_moe_wsel_b_none_p_kernel(
 
         w1w_first = keep.tile([P, G * H], I32, name="w1w_first", align_bytes=64)
         nc.vector.tensor_copy(w1w_first[:].bitcast(U32), w1w_all[0][:].bitcast(U32).indirect(list1[:]))
-        w1w = {}
+
+        h_sum = {}
         for r in range(G):
-            w1w[0, r] = w1w_first[:, r * H : (r + 1) * H]
+            for half in range(HALVES):
+                h_sum[r, half] = psum.tile([P, H], F32, name="h_sum", tag="bank%d" % (r * HALVES + half))
+
+        def first_product(r):
             second = keep.tile([P, H], I32, name="w1w_second%d" % r, align_bytes=64)
             nc.vector.tensor_copy(
                 second[:].bitcast(U32),
                 w1w_all[1][:].bitcast(U32).indirect(list1[:, r * H // 16 : (r + 1) * H // 16]),
             )
-            w1w[1, r] = second[:]
-        nc.vector.tensor_copy(w2s[:], w2s_all[:].indirect(list2[:]))
-
-        turned = []
-        h_toks = []
-        for r in range(G):
+            picked = [w1w_first[:, r * H : (r + 1) * H], second[:]]
             for half in range(HALVES):
                 tok = slice(half * P, (half + 1) * P)
-                col = r * HALVES + half
-                h_sum = psum.tile([P, H], F32, name="h_sum", tag="bank%d" % col)
                 for s in range(PASSES):
                     nc.tensor.matmul_mx(
-                        out=h_sum[:],
+                        out=h_sum[r, half][:],
                         lhsT=xw[:, s, tok].bitcast(FP8X4),
                         lhsT_scale=xs[4 * s : P, tok],
-                        rhs=w1w[s, r].bitcast(FP8X4),
+                        rhs=picked[s].bitcast(FP8X4),
                         rhs_scale=w1s[4 * s : P, r * H : (r + 1) * H],
                         start=(s == 0),
                         stop=(s == PASSES - 1),
                     )
-                if half == 0:
-                    turned.append(h_sum[:].rearrange("p (h u t) -> p h u t", h=HALVES, u=2))
+
+        def turned(r):
+            return h_sum[r, 0][:].rearrange("p (h u t) -> p h u t", h=HALVES, u=2)
+
+        def gate_and_turn(r):
+            h_toks = []
+            for half in range(HALVES):
+                col = r * HALVES + half
                 h_tok = work.tile([P, H], BF16, name="h_tok", bufs=G * HALVES, align_bytes=64)
                 nc.scalar.activation(
                     h_tok[:].rearrange("t (u p e) -> t u p e", u=2, e=2),
-                    h_sum[:].rearrange("t (p u e) -> t u p e", u=2, e=2),
+                    h_sum[r, half][:].rearrange("t (p u e) -> t u p e", u=2, e=2),
                     COPY,
                     scale=gate_cols[:, col : col + 1],
                 )
                 h_toks.append(h_tok)
-        for r in range(G):
             for half in range(HALVES):
-                words = h_toks[r * HALVES + half][:].bitcast(F32)
+                words = h_toks[half][:].bitcast(F32)
                 for u in range(2):
-                    nc.tensor.transpose(turned[r][:, half, u, :], words[:, u * P : (u + 1) * P], ident[:])
+                    nc.tensor.transpose(turned(r)[:, half, u, :], words[:, u * P : (u + 1) * P], ident[:])
 
-        acc = [psum.tile([P, H], F32, name="acc%d" % b, tag="bank%d" % (2 * b + 1)) for b in range(N // P)]
-        for r in range(G):
+        def quantise(r):
             h_in = work.tile([P, 4 * T], BF16, name="h_in", bufs=4, align_bytes=64)
             nc.scalar.copy(
                 h_in[:].bitcast(F32).rearrange("p (h t u) -> p h t u", h=HALVES, u=2),
-                turned[r].rearrange("p h u t -> p h t u"),
-            )
-            w2w = keep.tile([P, N], I32, name="w2w_%d" % r, align_bytes=64)
-            nc.vector.tensor_copy(
-                w2w[:].bitcast(U32),
-                w2w_all[:].bitcast(U32).indirect(list2[:, r * N // 16 : (r + 1) * N // 16]),
+                turned(r).rearrange("p h u t -> p h t u"),
             )
             h_codes = work.tile([P, T], U32, name="h_codes", bufs=4, align_bytes=64)
             h_scales = work.tile([P, T], U8, name="h_scales", bufs=4, align_bytes=64)
             nc.vector.quantize_mx(out=h_codes[:].bitcast(FP8X4), scales=h_scales[:], in_=h_in[:])
+            return h_codes, h_scales
+
+        def second_product(r, h_codes, h_scales):
             for b in range(N // P):
                 cols = slice(r * N + b * P, r * N + (b + 1) * P)
                 nc.tensor.matmul_mx(
                     out=acc[b][:, 0:T],
-                    lhsT=w2w[:, b * P : (b + 1) * P].bitcast(FP8X4),
+                    lhsT=w2w[r][:, b * P : (b + 1) * P].bitcast(FP8X4),
                     lhsT_scale=w2s[:, cols],
                     rhs=h_codes[:].bitcast(FP8X4),
                     rhs_scale=h_scales[:],
                     start=(r == 0),
                     stop=(r == G - 1),
                 )
+
+        for r in range(G):
+            first_product(r)
+            if r > 0:
+                gate_and_turn(r - 1)
+
+        nc.vector.tensor_copy(w2s[:], w2s_all[:].indirect(list2[:]))
+        w2w = []
+        for r in range(G):
+            picked = keep.tile([P, N], I32, name="w2w_%d" % r, align_bytes=64)
+            nc.vector.tensor_copy(
+                picked[:].bitcast(U32),
+                w2w_all[:].bitcast(U32).indirect(list2[:, r * N // 16 : (r + 1) * N // 16]),
+            )
+            w2w.append(picked)
+
+        early = [quantise(r) for r in range(G - 2)]
+        gate_and_turn(G - 1)
+        acc = [psum.tile([P, H], F32, name="acc%d" % b, tag="bank%d" % (G * HALVES - 1 - 2 * b)) for b in range(N // P)]
+        for r in range(G):
+            second_product(r, *(early[r] if r < G - 2 else quantise(r)))
 
         res = [keep.tile([P, T], F32, name="res%d" % b) for b in range(N // P)]
         nc.scalar.copy(res[0][:], acc[0][:, 0:T])

@@ -40,7 +40,7 @@ def tile_moe_wsel_b_none_p_kernel(
         xw = keep.tile([P, PASSES, T], I32, name="xw", align_bytes=64)
         xs = keep.tile([P, T], U8, name="xs", align_bytes=64)
         w1s_picked = keep.tile([P, G * H], U8, name="w1s_picked", align_bytes=64)
-        w1s = keep.tile([P, G * H], U8, name="w1s", align_bytes=64)
+        w1s = [keep.tile([P, G * H], U8, name="w1s%d" % s, align_bytes=64) for s in range(PASSES)]
         w2s = keep.tile([P, G * N], U8, name="w2s", align_bytes=64)
         gate_rows = keep.tile([P, P], F32, name="gate_rows")
         gate_cols = keep.tile([P, G * HALVES], F32, name="gate_cols")
@@ -48,7 +48,8 @@ def tile_moe_wsel_b_none_p_kernel(
 
         nc.vector.memset(w1s_all[0:STAGE, :].bitcast(I32), 0)
         nc.vector.memset(xs[:].bitcast(I32), 0)
-        nc.vector.memset(w1s[:].bitcast(I32), 0)
+        for s in range(PASSES):
+            nc.vector.memset(w1s[s][:].bitcast(I32), 0)
         nc.gpsimd.memset(gate_rows[:], 0.0)
         make_identity(nc, ident[:])
         nc.gpsimd.memset(w2s_all[:].bitcast(I32), 0)
@@ -63,15 +64,15 @@ def tile_moe_wsel_b_none_p_kernel(
                 x_scales[:, 4 * q : 4 * q + 4, :].bitcast(I32),
             )
         nc.sync.dma_start(xw[:], x_words.rearrange("s p t d -> p s (t d)").bitcast(I32))
-        nc.sync.dma_start(w1w_all[1][:], w1_words[1].rearrange("p m d -> p (m d)").bitcast(I32))
-
         nc.vector.tensor_copy(w1s_picked[:], w1s_all[:].indirect(list1[:]))
+        second_words = w1_words[1].rearrange("p m d -> p (m d)").bitcast(I32)
         for s in range(PASSES):
+            part = slice(s * E * H // PASSES, (s + 1) * E * H // PASSES)
+            nc.sync.dma_start(w1w_all[1][:, part], second_words[:, part])
             for j in range(4):
                 first = STAGE + 16 * s + j
-                queue = nc.gpsimd if (s, j) == (PASSES - 1, 3) else nc.sync
-                queue.dma_start(
-                    w1s[4 * s + j : P : 32, :].bitcast(I32),
+                nc.sync.dma_start(
+                    w1s[s][4 * s + j : P : 32, :].bitcast(I32),
                     w1s_picked[first : first + 13 : 4, :].bitcast(I32),
                 )
         nc.sync.dma_start(list2[:], offs2)
@@ -83,33 +84,36 @@ def tile_moe_wsel_b_none_p_kernel(
         nc.tensor.transpose(gate_t[:, 0:P], gate_rows[:], ident[:])
         nc.scalar.activation(gate_cols[:], gate_t[:, 0 : G * HALVES], COPY)
 
-        w1w_first = keep.tile([P, G * H], I32, name="w1w_first", align_bytes=64)
-        nc.vector.tensor_copy(w1w_first[:].bitcast(U32), w1w_all[0][:].bitcast(U32).indirect(list1[:]))
-
         h_sum = {}
         for r in range(G):
             for half in range(HALVES):
                 h_sum[r, half] = psum.tile([P, H], F32, name="h_sum", tag="bank%d" % (r * HALVES + half))
 
-        def first_product(r):
-            second = keep.tile([P, H], I32, name="w1w_second%d" % r, align_bytes=64)
-            nc.vector.tensor_copy(
-                second[:].bitcast(U32),
-                w1w_all[1][:].bitcast(U32).indirect(list1[:, r * H // 16 : (r + 1) * H // 16]),
-            )
-            picked = [w1w_first[:, r * H : (r + 1) * H], second[:]]
+        def first_product(s, r, picked):
             for half in range(HALVES):
                 tok = slice(half * P, (half + 1) * P)
-                for s in range(PASSES):
-                    nc.tensor.matmul_mx(
-                        out=h_sum[r, half][:],
-                        lhsT=xw[:, s, tok].bitcast(FP8X4),
-                        lhsT_scale=xs[4 * s : P, tok],
-                        rhs=picked[s].bitcast(FP8X4),
-                        rhs_scale=w1s[4 * s : P, r * H : (r + 1) * H],
-                        start=(s == 0),
-                        stop=(s == PASSES - 1),
-                    )
+                nc.tensor.matmul_mx(
+                    out=h_sum[r, half][:],
+                    lhsT=xw[:, s, tok].bitcast(FP8X4),
+                    lhsT_scale=xs[4 * s : P, tok],
+                    rhs=picked.bitcast(FP8X4),
+                    rhs_scale=w1s[s][4 * s : P, r * H : (r + 1) * H],
+                    start=(s == 0),
+                    stop=(s == PASSES - 1),
+                )
+
+        def gather_w1(s, r, count):
+            picked = keep.tile([P, count * H], I32, name="w1w_%d_%d" % (s, r), align_bytes=64)
+            nc.vector.tensor_copy(
+                picked[:].bitcast(U32),
+                w1w_all[s][:].bitcast(U32).indirect(list1[:, r * H // 16 : (r + count) * H // 16]),
+            )
+            return picked
+
+        for r in range(0, G, 2):
+            picked = gather_w1(0, r, 2)
+            for i in range(2):
+                first_product(0, r + i, picked[:, i * H : (i + 1) * H])
 
         def turned(r):
             return h_sum[r, 0][:].rearrange("p (h u t) -> p h u t", h=HALVES, u=2)
@@ -156,7 +160,7 @@ def tile_moe_wsel_b_none_p_kernel(
                 )
 
         for r in range(G):
-            first_product(r)
+            first_product(1, r, gather_w1(1, r, 1)[:])
             if r > 0:
                 gate_and_turn(r - 1)
 

@@ -20,6 +20,7 @@ PASSES = K // 512
 QUADS = 4
 HALVES = T // P
 STAGE = P - 16 * PASSES
+ORDER = (1, 0)
 
 
 def tile_moe_wsel_b_none_p_kernel(
@@ -37,7 +38,7 @@ def tile_moe_wsel_b_none_p_kernel(
         w2s_all = keep.tile([P, E * N], U8, name="w2s_all", align_bytes=64)
         w1w_all = [keep.tile([P, E * H], I32, name="w1w_all%d" % s, align_bytes=64) for s in range(PASSES)]
         w2w_all = keep.tile([P, E * N], I32, name="w2w_all", align_bytes=64)
-        xw = keep.tile([P, PASSES, T], I32, name="xw", align_bytes=64)
+        xw = [keep.tile([P, T], I32, name="xw%d" % s, align_bytes=64) for s in range(PASSES)]
         xs = keep.tile([P, T], U8, name="xs", align_bytes=64)
         w1s_picked = keep.tile([P, G * H], U8, name="w1s_picked", align_bytes=64)
         w1s = [keep.tile([P, G * H], U8, name="w1s%d" % s, align_bytes=64) for s in range(PASSES)]
@@ -56,23 +57,25 @@ def tile_moe_wsel_b_none_p_kernel(
 
         nc.sync.dma_start(w1s_all[STAGE:P, :].bitcast(I32), w1_scales.rearrange("s b m -> (s b) m").bitcast(I32))
         nc.sync.dma_start(list1[:], offs)
-        nc.sync.dma_start(w1w_all[0][:], w1_words[0].rearrange("p m d -> p (m d)").bitcast(I32))
+        nc.sync.dma_start(w1w_all[0][:], w1_words[ORDER[0]].rearrange("p m d -> p (m d)").bitcast(I32))
         nc.sync.dma_start(gate_rows[0 : G * HALVES, :], gate[:, 0, :].rearrange("r (h c) -> r h c", h=HALVES))
         for q in range(QUADS):
             nc.sync.dma_start(
                 xs[32 * q : 32 * q + 4 * PASSES, :].bitcast(I32),
                 x_scales[:, 4 * q : 4 * q + 4, :].bitcast(I32),
             )
-        nc.sync.dma_start(xw[:], x_words.rearrange("s p t d -> p s (t d)").bitcast(I32))
+        nc.sync.dma_start(xw[0][:], x_words[ORDER[0]].rearrange("p t d -> p (t d)").bitcast(I32))
         nc.vector.tensor_copy(w1s_picked[:], w1s_all[:].indirect(list1[:]))
-        second_words = w1_words[1].rearrange("p m d -> p (m d)").bitcast(I32)
+        second_words = w1_words[ORDER[1]].rearrange("p m d -> p (m d)").bitcast(I32)
         for s in range(PASSES):
             part = slice(s * E * H // PASSES, (s + 1) * E * H // PASSES)
             nc.sync.dma_start(w1w_all[1][:, part], second_words[:, part])
+            if s == 1:
+                nc.sync.dma_start(xw[1][:], x_words[ORDER[1]].rearrange("p t d -> p (t d)").bitcast(I32))
             for j in range(4):
-                first = STAGE + 16 * s + j
+                first = STAGE + 16 * ORDER[s] + j
                 nc.sync.dma_start(
-                    w1s[s][4 * s + j : P : 32, :].bitcast(I32),
+                    w1s[s][4 * ORDER[s] + j : P : 32, :].bitcast(I32),
                     w1s_picked[first : first + 13 : 4, :].bitcast(I32),
                 )
         nc.sync.dma_start(list2[:], offs2)
@@ -94,10 +97,10 @@ def tile_moe_wsel_b_none_p_kernel(
                 tok = slice(half * P, (half + 1) * P)
                 nc.tensor.matmul_mx(
                     out=h_sum[r, half][:],
-                    lhsT=xw[:, s, tok].bitcast(FP8X4),
-                    lhsT_scale=xs[4 * s : P, tok],
+                    lhsT=xw[s][:, tok].bitcast(FP8X4),
+                    lhsT_scale=xs[4 * ORDER[s] : P, tok],
                     rhs=picked.bitcast(FP8X4),
-                    rhs_scale=w1s[s][4 * s : P, r * H : (r + 1) * H],
+                    rhs_scale=w1s[s][4 * ORDER[s] : P, r * H : (r + 1) * H],
                     start=(s == 0),
                     stop=(s == PASSES - 1),
                 )
@@ -111,9 +114,9 @@ def tile_moe_wsel_b_none_p_kernel(
             return picked
 
         for r in range(0, G, 2):
-            picked = gather_w1(0, r, 2)
+            picked_first = gather_w1(0, r, 2)
             for i in range(2):
-                first_product(0, r + i, picked[:, i * H : (i + 1) * H])
+                first_product(0, r + i, picked_first[:, i * H : (i + 1) * H])
 
         def turned(r):
             return h_sum[r, 0][:].rearrange("p (h u t) -> p h u t", h=HALVES, u=2)
@@ -174,7 +177,21 @@ def tile_moe_wsel_b_none_p_kernel(
             )
             w2w.append(picked)
 
-        early = [quantise(r) for r in range(G - 2)]
+        early = []
+        for r in range(G - 2):
+            early.append(quantise(r))
+            idle = psum.tile([P, H], F32, name="idle", tag="bank%d" % (r * HALVES))
+            for half in range(HALVES):
+                tok = slice(half * P, (half + 1) * P)
+                nc.tensor.matmul_mx(
+                    out=idle[:],
+                    lhsT=xw[0][:, tok].bitcast(FP8X4),
+                    lhsT_scale=xs[4 * ORDER[0] : P, tok],
+                    rhs=picked_first[:, 0:H].bitcast(FP8X4),
+                    rhs_scale=w1s[0][4 * ORDER[0] : P, 2 * H : 3 * H],
+                    start=True,
+                    stop=True,
+                )
         gate_and_turn(G - 1)
         acc = [psum.tile([P, H], F32, name="acc%d" % b, tag="bank%d" % (G * HALVES - 1 - 2 * b)) for b in range(N // P)]
         for r in range(G):

@@ -42,6 +42,7 @@ def tile_moe_wsel_b_none_p_kernel(
         xs = keep.tile([P, T], U8, name="xs", align_bytes=64)
         w1s_picked = keep.tile([P, G * H], U8, name="w1s_picked", align_bytes=64)
         w1s = [keep.tile([P, G * H], U8, name="w1s%d" % s, align_bytes=64) for s in range(PASSES)]
+        w2s_picked = keep.tile([P, G * N], U8, name="w2s_picked", align_bytes=64)
         w2s = keep.tile([P, G * N], U8, name="w2s", align_bytes=64)
         gate_rows = keep.tile([P, P], F32, name="gate_rows")
         gate_cols = keep.tile([P, G * HALVES], F32, name="gate_cols")
@@ -54,18 +55,22 @@ def tile_moe_wsel_b_none_p_kernel(
         nc.gpsimd.memset(gate_rows[:], 0.0)
         make_identity(nc, ident[:])
         nc.gpsimd.memset(w2s_all[:].bitcast(I32), 0)
+        nc.vector.memset(w2s[:].bitcast(I32), 0)
 
         nc.sync.dma_start(w1s_all[STAGE:P, :].bitcast(I32), w1_scales.rearrange("s b m -> (s b) m").bitcast(I32))
         nc.sync.dma_start(list1[:], offs)
+        nc.sync.dma_start(list2[:], offs2)
+        nc.sync.dma_start(xw[0][:], x_words[ORDER[0]].rearrange("p t d -> p (t d)").bitcast(I32))
         nc.sync.dma_start(w1w_all[0][:], w1_words[ORDER[0]].rearrange("p m d -> p (m d)").bitcast(I32))
+        nc.sync.dma_start(w2s_all[32:64:2, :].bitcast(I32), w2_scales[0].bitcast(I32))
         nc.sync.dma_start(gate_rows[0 : G * HALVES, :], gate[:, 0, :].rearrange("r (h c) -> r h c", h=HALVES))
         for q in range(QUADS):
             nc.sync.dma_start(
                 xs[32 * q : 32 * q + 4 * PASSES, :].bitcast(I32),
                 x_scales[:, 4 * q : 4 * q + 4, :].bitcast(I32),
             )
-        nc.sync.dma_start(xw[0][:], x_words[ORDER[0]].rearrange("p t d -> p (t d)").bitcast(I32))
         nc.vector.tensor_copy(w1s_picked[:], w1s_all[:].indirect(list1[:]))
+        nc.vector.tensor_copy(w2s_picked[:], w2s_all[:].indirect(list2[:]))
         second_words = w1_words[ORDER[1]].rearrange("p m d -> p (m d)").bitcast(I32)
         for s in range(PASSES):
             part = slice(s * E * H // PASSES, (s + 1) * E * H // PASSES)
@@ -78,10 +83,9 @@ def tile_moe_wsel_b_none_p_kernel(
                     w1s[s][4 * ORDER[s] + j : P : 32, :].bitcast(I32),
                     w1s_picked[first : first + 13 : 4, :].bitcast(I32),
                 )
-        nc.sync.dma_start(list2[:], offs2)
-        for j in range(4):
-            nc.sync.dma_start(w2s_all[j:P:32, :].bitcast(I32), w2_scales[0, j:16:4, :].bitcast(I32))
         nc.sync.dma_start(w2w_all[:], w2_words[0].rearrange("p m d -> p (m d)").bitcast(I32))
+        for j in range(4):
+            nc.sync.dma_start(w2s[j:P:32, :].bitcast(I32), w2s_picked[32 + 2 * j : 64 : 8, :].bitcast(I32))
 
         gate_t = psum.tile([P, H], F32, name="gate_t", tag="bank%d" % (G * HALVES - 1))
         nc.tensor.transpose(gate_t[:, 0:P], gate_rows[:], ident[:])
@@ -140,21 +144,26 @@ def tile_moe_wsel_b_none_p_kernel(
 
         def quantise(r):
             h_in = work.tile([P, 4 * T], BF16, name="h_in", bufs=4, align_bytes=64)
-            nc.scalar.copy(
+            (nc.vector.tensor_copy if r == 1 else nc.scalar.copy)(
                 h_in[:].bitcast(F32).rearrange("p (h t u) -> p h t u", h=HALVES, u=2),
                 turned(r).rearrange("p h u t -> p h t u"),
+            )
+            w2w = keep.tile([P, N], I32, name="w2w_%d" % r, align_bytes=64)
+            nc.vector.tensor_copy(
+                w2w[:].bitcast(U32),
+                w2w_all[:].bitcast(U32).indirect(list2[:, r * N // 16 : (r + 1) * N // 16]),
             )
             h_codes = work.tile([P, T], U32, name="h_codes", bufs=4, align_bytes=64)
             h_scales = work.tile([P, T], U8, name="h_scales", bufs=4, align_bytes=64)
             nc.vector.quantize_mx(out=h_codes[:].bitcast(FP8X4), scales=h_scales[:], in_=h_in[:])
-            return h_codes, h_scales
+            return w2w, h_codes, h_scales
 
-        def second_product(r, h_codes, h_scales):
+        def second_product(r, w2w, h_codes, h_scales):
             for b in range(N // P):
                 cols = slice(r * N + b * P, r * N + (b + 1) * P)
                 nc.tensor.matmul_mx(
                     out=acc[b][:, 0:T],
-                    lhsT=w2w[r][:, b * P : (b + 1) * P].bitcast(FP8X4),
+                    lhsT=w2w[:, b * P : (b + 1) * P].bitcast(FP8X4),
                     lhsT_scale=w2s[:, cols],
                     rhs=h_codes[:].bitcast(FP8X4),
                     rhs_scale=h_scales[:],
@@ -166,36 +175,21 @@ def tile_moe_wsel_b_none_p_kernel(
             first_product(1, r, gather_w1(1, r, 1)[:])
             if r > 0:
                 gate_and_turn(r - 1)
-
-        nc.vector.tensor_copy(w2s[:], w2s_all[:].indirect(list2[:]))
-        w2w = []
-        for r in range(G):
-            picked = keep.tile([P, N], I32, name="w2w_%d" % r, align_bytes=64)
-            nc.vector.tensor_copy(
-                picked[:].bitcast(U32),
-                w2w_all[:].bitcast(U32).indirect(list2[:, r * N // 16 : (r + 1) * N // 16]),
-            )
-            w2w.append(picked)
-
-        early = []
-        for r in range(G - 2):
-            early.append(quantise(r))
-            idle = psum.tile([P, H], F32, name="idle", tag="bank%d" % (r * HALVES))
-            for half in range(HALVES):
-                tok = slice(half * P, (half + 1) * P)
-                nc.tensor.matmul_mx(
-                    out=idle[:],
-                    lhsT=xw[0][:, tok].bitcast(FP8X4),
-                    lhsT_scale=xs[4 * ORDER[0] : P, tok],
-                    rhs=picked_first[:, 0:H].bitcast(FP8X4),
-                    rhs_scale=w1s[0][4 * ORDER[0] : P, 2 * H : 3 * H],
-                    start=True,
-                    stop=True,
-                )
+        idle = psum.tile([P, H], F32, name="idle", tag="bank5")
         gate_and_turn(G - 1)
-        acc = [psum.tile([P, H], F32, name="acc%d" % b, tag="bank%d" % (G * HALVES - 1 - 2 * b)) for b in range(N // P)]
+        for i in range(4):
+            nc.tensor.matmul_mx(
+                out=idle[:],
+                lhsT=xw[0][:, 0:P].bitcast(FP8X4),
+                lhsT_scale=xs[4 * ORDER[0] : P, 0:P],
+                rhs=picked_first[:, 0:H].bitcast(FP8X4),
+                rhs_scale=w1s[0][4 * ORDER[0] : P, 2 * H : 3 * H],
+                start=(i == 0),
+                stop=(i == 3),
+            )
+        acc = [psum.tile([P, H], F32, name="acc%d" % b, tag="bank%d" % (2 * b + 1)) for b in range(N // P)]
         for r in range(G):
-            second_product(r, *(early[r] if r < G - 2 else quantise(r)))
+            second_product(r, *quantise(r))
 
         res = [keep.tile([P, T], F32, name="res%d" % b) for b in range(N // P)]
         nc.scalar.copy(res[0][:], acc[0][:, 0:T])

@@ -14,6 +14,7 @@ U16 = mybir.dt.uint16
 U8 = mybir.dt.uint8
 FP8X4 = mybir.dt.float8_e4m3fn_x4
 COPY = mybir.ActivationFunctionType.Copy
+MULT = mybir.AluOpType.mult
 
 P = 128
 PASSES = K // 512
@@ -125,38 +126,43 @@ def tile_moe_wsel_b_none_p_kernel(
         def turned(r):
             return h_sum[r, 0][:].rearrange("p (h u t) -> p h u t", h=HALVES, u=2)
 
-        def gate_and_turn(r):
-            h_toks = []
-            for half in range(HALVES):
-                col = r * HALVES + half
-                h_tok = work.tile([P, H], BF16, name="h_tok", bufs=G * HALVES, align_bytes=64)
-                nc.scalar.activation(
-                    h_tok[:].rearrange("t (u p e) -> t u p e", u=2, e=2),
-                    h_sum[r, half][:].rearrange("t (p u e) -> t u p e", u=2, e=2),
-                    COPY,
-                    scale=gate_cols[:, col : col + 1],
-                )
-                h_toks.append(h_tok)
-            for half in range(HALVES):
-                words = h_toks[half][:].bitcast(F32)
-                for u in range(2):
-                    nc.tensor.transpose(turned(r)[:, half, u, :], words[:, u * P : (u + 1) * P], ident[:])
+        def gated_copy(r, half):
+            col = r * HALVES + half
+            h_tok = work.tile([P, H], BF16, name="h_tok", bufs=G * HALVES, align_bytes=64)
+            dst = h_tok[:].rearrange("t (u p e) -> t u p e", u=2, e=2)
+            src = h_sum[r, half][:].rearrange("t (p u e) -> t u p e", u=2, e=2)
+            if half == 1 and r > 0:
+                nc.vector.tensor_scalar(dst, src, gate_cols[:, col : col + 1], None, MULT)
+            else:
+                nc.scalar.activation(dst, src, COPY, scale=gate_cols[:, col : col + 1])
+            return h_tok
 
-        def quantise(r):
+        def turn(r, half, h_tok):
+            words = h_tok[:].bitcast(F32)
+            for u in range(2):
+                nc.tensor.transpose(turned(r)[:, half, u, :], words[:, u * P : (u + 1) * P], ident[:])
+
+        def turned_copy(r):
             h_in = work.tile([P, 4 * T], BF16, name="h_in", bufs=4, align_bytes=64)
-            (nc.vector.tensor_copy if r == 1 else nc.scalar.copy)(
+            nc.scalar.copy(
                 h_in[:].bitcast(F32).rearrange("p (h t u) -> p h t u", h=HALVES, u=2),
                 turned(r).rearrange("p h u t -> p h t u"),
             )
+            return h_in
+
+        def gather_w2(r):
             w2w = keep.tile([P, N], I32, name="w2w_%d" % r, align_bytes=64)
             nc.vector.tensor_copy(
                 w2w[:].bitcast(U32),
                 w2w_all[:].bitcast(U32).indirect(list2[:, r * N // 16 : (r + 1) * N // 16]),
             )
+            return w2w
+
+        def quantise(h_in):
             h_codes = work.tile([P, T], U32, name="h_codes", bufs=4, align_bytes=64)
             h_scales = work.tile([P, T], U8, name="h_scales", bufs=4, align_bytes=64)
             nc.vector.quantize_mx(out=h_codes[:].bitcast(FP8X4), scales=h_scales[:], in_=h_in[:])
-            return w2w, h_codes, h_scales
+            return h_codes, h_scales
 
         def second_product(r, w2w, h_codes, h_scales):
             for b in range(N // P):
@@ -173,10 +179,12 @@ def tile_moe_wsel_b_none_p_kernel(
 
         for r in range(G):
             first_product(1, r, gather_w1(1, r, 1)[:])
-            if r > 0:
-                gate_and_turn(r - 1)
-        idle = psum.tile([P, H], F32, name="idle", tag="bank5")
-        gate_and_turn(G - 1)
+        h_toks = {(r, half): gated_copy(r, half) for r in range(G) for half in range(HALVES)}
+        for r in range(G):
+            for half in range(HALVES):
+                turn(r, half, h_toks[r, half])
+        h_ins = [turned_copy(r) for r in range(G)]
+        idle = psum.tile([P, H], F32, name="idle", tag="bank0")
         for i in range(4):
             nc.tensor.matmul_mx(
                 out=idle[:],
@@ -189,7 +197,8 @@ def tile_moe_wsel_b_none_p_kernel(
             )
         acc = [psum.tile([P, H], F32, name="acc%d" % b, tag="bank%d" % (2 * b + 1)) for b in range(N // P)]
         for r in range(G):
-            second_product(r, *quantise(r))
+            w2w = gather_w2(r)
+            second_product(r, w2w, *quantise(h_ins[r]))
 
         res = [keep.tile([P, T], F32, name="res%d" % b) for b in range(N // P)]
         nc.scalar.copy(res[0][:], acc[0][:, 0:T])

@@ -49,14 +49,17 @@ def tile_moe_wsel_b_none_p_kernel(
         gate_cols = keep.tile([P, G * HALVES], F32, name="gate_cols")
         ident = keep.tile([P, P], F32, name="ident")
 
+        def gather(dst, window, offsets, first, count):
+            nc.vector.tensor_copy(dst, window.indirect(offsets[:, first // 16 : (first + count) // 16]))
+
         nc.vector.memset(w1s_all[0:STAGE, :].bitcast(I32), 0)
         nc.vector.memset(xs[:].bitcast(I32), 0)
-        for s in range(PASSES):
-            nc.vector.memset(w1s[s][:].bitcast(I32), 0)
+        nc.vector.memset(w1s[0][:].bitcast(I32), 0)
         nc.gpsimd.memset(gate_rows[:], 0.0)
         make_identity(nc, ident[:])
         nc.gpsimd.memset(w2s_all[:].bitcast(I32), 0)
-        nc.vector.memset(w2s[:].bitcast(I32), 0)
+        nc.gpsimd.memset(w1s[1][:].bitcast(I32), 0)
+        nc.gpsimd.memset(w2s[:].bitcast(I32), 0)
 
         nc.sync.dma_start(w1s_all[STAGE:P, :].bitcast(I32), w1_scales.rearrange("s b m -> (s b) m").bitcast(I32))
         nc.sync.dma_start(list1[:], offs)
@@ -70,8 +73,8 @@ def tile_moe_wsel_b_none_p_kernel(
                 xs[32 * q : 32 * q + 4 * PASSES, :].bitcast(I32),
                 x_scales[:, 4 * q : 4 * q + 4, :].bitcast(I32),
             )
-        nc.vector.tensor_copy(w1s_picked[:], w1s_all[:].indirect(list1[:]))
-        nc.vector.tensor_copy(w2s_picked[:], w2s_all[:].indirect(list2[:]))
+        gather(w1s_picked[:], w1s_all[:], list1, 0, G * H)
+        gather(w2s_picked[:], w2s_all[:], list2, 0, G * N)
         second_words = w1_words[ORDER[1]].rearrange("p m d -> p (m d)").bitcast(I32)
         for s in range(PASSES):
             part = slice(s * E * H // PASSES, (s + 1) * E * H // PASSES)
@@ -92,6 +95,27 @@ def tile_moe_wsel_b_none_p_kernel(
         nc.tensor.transpose(gate_t[:, 0:P], gate_rows[:], ident[:])
         nc.scalar.activation(gate_cols[:], gate_t[:, 0 : G * HALVES], COPY)
 
+        def warm_up(bank, words):
+            idle = psum.tile([P, H], F32, name="idle", tag="bank%d" % bank)
+            for i in range(2):
+                nc.tensor.matmul_mx(
+                    out=idle[:],
+                    lhsT=xw[0][:, 0:P].bitcast(FP8X4),
+                    lhsT_scale=xs[4 * ORDER[0] : P, 0:P],
+                    rhs=words[:, 0:H].bitcast(FP8X4),
+                    rhs_scale=w1s_picked[4 * ORDER[0] : P, 0:H],
+                    start=(i == 0),
+                    stop=(i == 1),
+                )
+
+        def gather_w1(s, r, count):
+            picked = keep.tile([P, count * H], I32, name="w1w_%d_%d" % (s, r), align_bytes=64)
+            gather(picked[:].bitcast(U32), w1w_all[s][:].bitcast(U32), list1, r * H, count * H)
+            return picked
+
+        picked_first = [gather_w1(0, r, 2) for r in range(0, G, 2)]
+        warm_up(G * HALVES - 2, picked_first[0])
+
         h_sum = {}
         for r in range(G):
             for half in range(HALVES):
@@ -110,18 +134,8 @@ def tile_moe_wsel_b_none_p_kernel(
                     stop=(s == PASSES - 1),
                 )
 
-        def gather_w1(s, r, count):
-            picked = keep.tile([P, count * H], I32, name="w1w_%d_%d" % (s, r), align_bytes=64)
-            nc.vector.tensor_copy(
-                picked[:].bitcast(U32),
-                w1w_all[s][:].bitcast(U32).indirect(list1[:, r * H // 16 : (r + count) * H // 16]),
-            )
-            return picked
-
-        for r in range(0, G, 2):
-            picked_first = gather_w1(0, r, 2)
-            for i in range(2):
-                first_product(0, r + i, picked_first[:, i * H : (i + 1) * H])
+        for r in range(G):
+            first_product(0, r, picked_first[r // 2][:, r % 2 * H : (r % 2 + 1) * H])
 
         def turned(r):
             return h_sum[r, 0][:].rearrange("p (h u t) -> p h u t", h=HALVES, u=2)
@@ -152,10 +166,7 @@ def tile_moe_wsel_b_none_p_kernel(
 
         def gather_w2(r):
             w2w = keep.tile([P, N], I32, name="w2w_%d" % r, align_bytes=64)
-            nc.vector.tensor_copy(
-                w2w[:].bitcast(U32),
-                w2w_all[:].bitcast(U32).indirect(list2[:, r * N // 16 : (r + 1) * N // 16]),
-            )
+            gather(w2w[:].bitcast(U32), w2w_all[:].bitcast(U32), list2, r * N, N)
             return w2w
 
         def quantise(h_in):
@@ -183,18 +194,9 @@ def tile_moe_wsel_b_none_p_kernel(
         for r in range(G):
             for half in range(HALVES):
                 turn(r, half, h_toks[r, half])
+            if r == G - 2:
+                warm_up(G * HALVES - 1, picked_first[0])
         h_ins = [turned_copy(r) for r in range(G)]
-        idle = psum.tile([P, H], F32, name="idle", tag="bank0")
-        for i in range(4):
-            nc.tensor.matmul_mx(
-                out=idle[:],
-                lhsT=xw[0][:, 0:P].bitcast(FP8X4),
-                lhsT_scale=xs[4 * ORDER[0] : P, 0:P],
-                rhs=picked_first[:, 0:H].bitcast(FP8X4),
-                rhs_scale=w1s[0][4 * ORDER[0] : P, 2 * H : 3 * H],
-                start=(i == 0),
-                stop=(i == 3),
-            )
         acc = [psum.tile([P, H], F32, name="acc%d" % b, tag="bank%d" % (2 * b + 1)) for b in range(N // P)]
         for r in range(G):
             w2w = gather_w2(r)

@@ -156,11 +156,11 @@ def tile_moe_wsel_b_none_p_kernel(
             for u in range(2):
                 nc.tensor.transpose(turned(r)[:, half, u, :], words[:, u * P : (u + 1) * P], ident[:])
 
-        def turned_copy(r):
-            h_in = work.tile([P, 4 * T], BF16, name="h_in", bufs=4, align_bytes=64)
+        def turned_copy(r, halves):
+            h_in = work.tile([P, 4 * P * len(halves)], BF16, name="h_in", bufs=G + 1, align_bytes=64)
             nc.scalar.copy(
-                h_in[:].bitcast(F32).rearrange("p (h t u) -> p h t u", h=HALVES, u=2),
-                turned(r).rearrange("p h u t -> p h t u"),
+                h_in[:].bitcast(F32).rearrange("p (h t u) -> p h t u", h=len(halves), u=2),
+                turned(r)[:, halves[0] : halves[-1] + 1].rearrange("p h u t -> p h t u"),
             )
             return h_in
 
@@ -169,24 +169,26 @@ def tile_moe_wsel_b_none_p_kernel(
             gather(w2w[:].bitcast(U32), w2w_all[:].bitcast(U32), list2, r * N, N)
             return w2w
 
-        def quantise(h_in):
-            h_codes = work.tile([P, T], U32, name="h_codes", bufs=4, align_bytes=64)
-            h_scales = work.tile([P, T], U8, name="h_scales", bufs=4, align_bytes=64)
+        def quantise(h_in, halves):
+            h_codes = work.tile([P, P * len(halves)], U32, name="h_codes", bufs=G + 1, align_bytes=64)
+            h_scales = work.tile([P, P * len(halves)], U8, name="h_scales", bufs=G + 1, align_bytes=64)
             nc.vector.quantize_mx(out=h_codes[:].bitcast(FP8X4), scales=h_scales[:], in_=h_in[:])
             return h_codes, h_scales
 
-        def second_product(r, w2w, h_codes, h_scales):
-            for b in range(N // P):
-                cols = slice(r * N + b * P, r * N + (b + 1) * P)
-                nc.tensor.matmul_mx(
-                    out=acc[b][:, 0:T],
-                    lhsT=w2w[:, b * P : (b + 1) * P].bitcast(FP8X4),
-                    lhsT_scale=w2s[:, cols],
-                    rhs=h_codes[:].bitcast(FP8X4),
-                    rhs_scale=h_scales[:],
-                    start=(r == 0),
-                    stop=(r == G - 1),
-                )
+        def second_product(r, halves, w2w, h_codes, h_scales):
+            for i, half in enumerate(halves):
+                tok = slice(i * P, (i + 1) * P)
+                for b in range(N // P):
+                    cols = slice(r * N + b * P, r * N + (b + 1) * P)
+                    nc.tensor.matmul_mx(
+                        out=acc[half, b][:, 0:P],
+                        lhsT=w2w[:, b * P : (b + 1) * P].bitcast(FP8X4),
+                        lhsT_scale=w2s[:, cols],
+                        rhs=h_codes[:, tok].bitcast(FP8X4),
+                        rhs_scale=h_scales[:, tok],
+                        start=(r == 0),
+                        stop=(r == G - 1),
+                    )
 
         for r in range(G):
             first_product(1, r, gather_w1(1, r, 1)[:])
@@ -196,14 +198,20 @@ def tile_moe_wsel_b_none_p_kernel(
                 turn(r, half, h_toks[r, half])
             if r == G - 2:
                 warm_up(G * HALVES - 1, picked_first[0])
-        h_ins = [turned_copy(r) for r in range(G)]
-        acc = [psum.tile([P, H], F32, name="acc%d" % b, tag="bank%d" % (2 * b + 1)) for b in range(N // P)]
-        for r in range(G):
-            w2w = gather_w2(r)
-            second_product(r, w2w, *quantise(h_ins[r]))
+        pieces = [(r, (0, 1)) for r in range(G - 1)] + [(G - 1, (0,)), (G - 1, (1,))]
+        h_ins = [turned_copy(r, halves) for r, halves in pieces]
+        acc = {}
+        for half in range(HALVES):
+            for b in range(N // P):
+                acc[half, b] = psum.tile([P, H], F32, name="acc", tag="bank%d" % (2 * (2 * half + b) + 1))
+        w2w = [gather_w2(r) for r in range(G)]
+        for (r, halves), h_in in zip(pieces, h_ins):
+            second_product(r, halves, w2w[r], *quantise(h_in, halves))
 
-        res = [keep.tile([P, T], F32, name="res%d" % b) for b in range(N // P)]
-        nc.scalar.copy(res[0][:], acc[0][:, 0:T])
-        nc.scalar.dma_start(out[0:P, :], res[0][:])
-        nc.vector.tensor_copy(res[1][:], acc[1][:, 0:T])
-        nc.sync.dma_start(out[P : 2 * P, :], res[1][:])
+        for half in range(HALVES):
+            res = keep.tile([P, N // P, P], F32, name="res%d" % half)
+            nc.vector.tensor_copy(res[:, 0, :], acc[half, 0][:, 0:P])
+            nc.scalar.copy(res[:, 1, :], acc[half, 1][:, 0:P])
+            (nc.sync if half == 0 else nc.scalar).dma_start(
+                out.rearrange("(b p) t -> p b t", p=P)[:, :, half * P : (half + 1) * P], res[:]
+            )

@@ -66,7 +66,7 @@ def tile_moe_wsel_b_none_p_kernel(
         nc.sync.dma_start(list2[:], offs2)
         nc.sync.dma_start(xw[0][:], x_words[ORDER[0]].rearrange("p t d -> p (t d)").bitcast(I32))
         nc.sync.dma_start(w1w_all[0][:], w1_words[ORDER[0]].rearrange("p m d -> p (m d)").bitcast(I32))
-        nc.sync.dma_start(w2s_all[32:64:2, :].bitcast(I32), w2_scales[0].bitcast(I32))
+        nc.sync.dma_start(w2s_all[32:96:4, :].bitcast(I32), w2_scales[0].bitcast(I32))
         nc.sync.dma_start(gate_rows[0 : G * HALVES, :], gate[:, 0, :].rearrange("r (h c) -> r h c", h=HALVES))
         for q in range(QUADS):
             nc.sync.dma_start(
@@ -76,20 +76,26 @@ def tile_moe_wsel_b_none_p_kernel(
         gather(w1s_picked[:], w1s_all[:], list1, 0, G * H)
         gather(w2s_picked[:], w2s_all[:], list2, 0, G * N)
         second_words = w1_words[ORDER[1]].rearrange("p m d -> p (m d)").bitcast(I32)
-        for s in range(PASSES):
-            part = slice(s * E * H // PASSES, (s + 1) * E * H // PASSES)
-            nc.sync.dma_start(w1w_all[1][:, part], second_words[:, part])
-            if s == 1:
-                nc.sync.dma_start(xw[1][:], x_words[ORDER[1]].rearrange("p t d -> p (t d)").bitcast(I32))
-            for j in range(4):
-                first = STAGE + 16 * ORDER[s] + j
-                nc.sync.dma_start(
-                    w1s[s][4 * ORDER[s] + j : P : 32, :].bitcast(I32),
-                    w1s_picked[first : first + 13 : 4, :].bitcast(I32),
-                )
+
+        def move_w1_scales(s, j):
+            first = STAGE + 16 * ORDER[s] + j
+            nc.sync.dma_start(
+                w1s[s][4 * ORDER[s] + j : P : 32, :].bitcast(I32),
+                w1s_picked[first : first + 13 : 4, :].bitcast(I32),
+            )
+
+        nc.sync.dma_start(w1w_all[1][:, 0 : E * H // 2], second_words[:, 0 : E * H // 2])
+        for j in range(4):
+            move_w1_scales(0, j)
+            if j < 2:
+                move_w1_scales(1, j)
+        nc.sync.dma_start(w1w_all[1][:, E * H // 2 : E * H], second_words[:, E * H // 2 : E * H])
+        nc.sync.dma_start(xw[1][:], x_words[ORDER[1]].rearrange("p t d -> p (t d)").bitcast(I32))
+        for j in range(2, 4):
+            move_w1_scales(1, j)
         nc.sync.dma_start(w2w_all[:], w2_words[0].rearrange("p m d -> p (m d)").bitcast(I32))
         for j in range(4):
-            nc.sync.dma_start(w2s[j:P:32, :].bitcast(I32), w2s_picked[32 + 2 * j : 64 : 8, :].bitcast(I32))
+            nc.sync.dma_start(w2s[j:P:32, :].bitcast(I32), w2s_picked[32 + 4 * j : 96 : 16, :].bitcast(I32))
 
         gate_t = psum.tile([P, H], F32, name="gate_t", tag="bank%d" % (G * HALVES - 1))
         nc.tensor.transpose(gate_t[:, 0:P], gate_rows[:], ident[:])

@@ -120,7 +120,6 @@ def tile_moe_wsel_b_none_p_kernel(
             return picked
 
         picked_first = [gather_w1(0, r, 2) for r in range(0, G, 2)]
-        warm_up(G * HALVES - 2, picked_first[0])
 
         h_sum = {}
         for r in range(G):

@@ -22,6 +22,7 @@ QUADS = 4
 HALVES = T // P
 STAGE = P - 16 * PASSES
 ORDER = (1, 0)
+CUT = 10 * E * H // 16
 
 
 def tile_moe_wsel_b_none_p_kernel(
@@ -43,6 +44,7 @@ def tile_moe_wsel_b_none_p_kernel(
         xs = keep.tile([P, T], U8, name="xs", align_bytes=64)
         w1s_picked = keep.tile([P, G * H], U8, name="w1s_picked", align_bytes=64)
         w1s = [keep.tile([P, G * H], U8, name="w1s%d" % s, align_bytes=64) for s in range(PASSES)]
+        lead_scales = keep.tile([P, H], U8, name="lead_scales", align_bytes=64)
         w2s_picked = keep.tile([P, G * N], U8, name="w2s_picked", align_bytes=64)
         w2s = keep.tile([P, G * N], U8, name="w2s", align_bytes=64)
         gate_rows = keep.tile([P, P], F32, name="gate_rows")
@@ -52,47 +54,55 @@ def tile_moe_wsel_b_none_p_kernel(
         def gather(dst, window, offsets, first, count):
             nc.vector.tensor_copy(dst, window.indirect(offsets[:, first // 16 : (first + count) // 16]))
 
-        nc.vector.memset(w1s_all[0:STAGE, :].bitcast(I32), 0)
         nc.vector.memset(xs[:].bitcast(I32), 0)
-        nc.vector.memset(w1s[0][:].bitcast(I32), 0)
-        nc.gpsimd.memset(gate_rows[:], 0.0)
-        make_identity(nc, ident[:])
+        nc.vector.memset(w1s_all[0:STAGE, :].bitcast(I32), 0)
+        nc.vector.memset(lead_scales[:].bitcast(I32), 0)
+        nc.vector.memset(w1s[0][:, H : G * H].bitcast(I32), 0)
+        nc.vector.memset(w1s[1][:].bitcast(I32), 0)
+        nc.vector.memset(w2s[:].bitcast(I32), 0)
         nc.gpsimd.memset(w2s_all[:].bitcast(I32), 0)
-        nc.gpsimd.memset(w1s[1][:].bitcast(I32), 0)
-        nc.gpsimd.memset(w2s[:].bitcast(I32), 0)
+        nc.gpsimd.memset(gate_rows[:], 0.0)
+        nc.gpsimd.dma_start(gate_rows[0 : G * HALVES, :], gate[:, 0, :].rearrange("r (h c) -> r h c", h=HALVES))
+        make_identity(nc, ident[:])
 
         nc.sync.dma_start(w1s_all[STAGE:P, :].bitcast(I32), w1_scales.rearrange("s b m -> (s b) m").bitcast(I32))
         nc.sync.dma_start(list1[:], offs)
-        nc.sync.dma_start(list2[:], offs2)
         nc.sync.dma_start(xw[0][:], x_words[ORDER[0]].rearrange("p t d -> p (t d)").bitcast(I32))
-        nc.sync.dma_start(w1w_all[0][:], w1_words[ORDER[0]].rearrange("p m d -> p (m d)").bitcast(I32))
-        nc.sync.dma_start(w2s_all[32:96:4, :].bitcast(I32), w2_scales[0].bitcast(I32))
-        nc.sync.dma_start(gate_rows[0 : G * HALVES, :], gate[:, 0, :].rearrange("r (h c) -> r h c", h=HALVES))
         for q in range(QUADS):
             nc.sync.dma_start(
                 xs[32 * q : 32 * q + 4 * PASSES, :].bitcast(I32),
                 x_scales[:, 4 * q : 4 * q + 4, :].bitcast(I32),
             )
-        gather(w1s_picked[:], w1s_all[:], list1, 0, G * H)
+        nc.sync.dma_start(w1w_all[0][:], w1_words[ORDER[0]].rearrange("p m d -> p (m d)").bitcast(I32))
+        nc.sync.dma_start(list2[:], offs2)
+        nc.sync.dma_start(w2s_all[32:96:4, :].bitcast(I32), w2_scales[0].bitcast(I32))
+        gather(w1s_picked[:, 0:H], w1s_all[:], list1, 0, H)
+        gather(w1s_picked[:, H : G * H], w1s_all[:], list1, H, (G - 1) * H)
         gather(w2s_picked[:], w2s_all[:], list2, 0, G * N)
         second_words = w1_words[ORDER[1]].rearrange("p m d -> p (m d)").bitcast(I32)
 
-        def move_w1_scales(s, j):
+        def move_w1_scales(s, j, cols):
             first = STAGE + 16 * ORDER[s] + j
             nc.sync.dma_start(
-                w1s[s][4 * ORDER[s] + j : P : 32, :].bitcast(I32),
-                w1s_picked[first : first + 13 : 4, :].bitcast(I32),
+                w1s[s][4 * ORDER[s] + j : P : 32, cols].bitcast(I32),
+                w1s_picked[first : first + 13 : 4, cols].bitcast(I32),
             )
 
-        nc.sync.dma_start(w1w_all[1][:, 0 : E * H // 2], second_words[:, 0 : E * H // 2])
+        for q in (0, 2, 1, 3):
+            first, row = STAGE + 16 * ORDER[0] + 4 * q, 32 * q + 4 * ORDER[0]
+            nc.sync.dma_start(
+                lead_scales[row : row + 4, :].bitcast(I32),
+                w1s_picked[first : first + 4, 0:H].bitcast(I32),
+            )
+        nc.sync.dma_start(w1w_all[1][:, 0:CUT], second_words[:, 0:CUT])
         for j in range(4):
-            move_w1_scales(0, j)
+            move_w1_scales(0, j, slice(H, G * H))
             if j < 2:
-                move_w1_scales(1, j)
-        nc.sync.dma_start(w1w_all[1][:, E * H // 2 : E * H], second_words[:, E * H // 2 : E * H])
+                move_w1_scales(1, j, slice(0, G * H))
+        nc.sync.dma_start(w1w_all[1][:, CUT : E * H], second_words[:, CUT : E * H])
         nc.sync.dma_start(xw[1][:], x_words[ORDER[1]].rearrange("p t d -> p (t d)").bitcast(I32))
         for j in range(2, 4):
-            move_w1_scales(1, j)
+            move_w1_scales(1, j, slice(0, G * H))
         nc.sync.dma_start(w2w_all[:], w2_words[0].rearrange("p m d -> p (m d)").bitcast(I32))
         for j in range(4):
             nc.sync.dma_start(w2s[j:P:32, :].bitcast(I32), w2s_picked[32 + 4 * j : 96 : 16, :].bitcast(I32))
@@ -109,7 +119,7 @@ def tile_moe_wsel_b_none_p_kernel(
                     lhsT=xw[0][:, 0:P].bitcast(FP8X4),
                     lhsT_scale=xs[4 * ORDER[0] : P, 0:P],
                     rhs=words[:, 0:H].bitcast(FP8X4),
-                    rhs_scale=w1s_picked[4 * ORDER[0] : P, 0:H],
+                    rhs_scale=lead_scales[4 * ORDER[0] : P, :],
                     start=(i == 0),
                     stop=(i == 1),
                 )
@@ -134,7 +144,7 @@ def tile_moe_wsel_b_none_p_kernel(
                     lhsT=xw[s][:, tok].bitcast(FP8X4),
                     lhsT_scale=xs[4 * ORDER[s] : P, tok],
                     rhs=picked.bitcast(FP8X4),
-                    rhs_scale=w1s[s][4 * ORDER[s] : P, r * H : (r + 1) * H],
+                    rhs_scale=(lead_scales if (s, r) == (0, 0) else w1s[s])[4 * ORDER[s] : P, r * H : (r + 1) * H],
                     start=(s == 0),
                     stop=(s == PASSES - 1),
                 )

@@ -22,7 +22,7 @@ QUADS = 4
 HALVES = T // P
 STAGE = P - 16 * PASSES
 ORDER = (1, 0)
-CUT = 10 * E * H // 16
+CUT = 9 * E * H // 16
 
 
 def tile_moe_wsel_b_none_p_kernel(
@@ -45,7 +45,6 @@ def tile_moe_wsel_b_none_p_kernel(
         w1s_picked = keep.tile([P, G * H], U8, name="w1s_picked", align_bytes=64)
         w1s = [keep.tile([P, G * H], U8, name="w1s%d" % s, align_bytes=64) for s in range(PASSES)]
         lead_scales = keep.tile([P, H], U8, name="lead_scales", align_bytes=64)
-        w2s_picked = keep.tile([P, G * N], U8, name="w2s_picked", align_bytes=64)
         w2s = keep.tile([P, G * N], U8, name="w2s", align_bytes=64)
         gate_rows = keep.tile([P, P], F32, name="gate_rows")
         gate_cols = keep.tile([P, G * HALVES], F32, name="gate_cols")
@@ -62,23 +61,26 @@ def tile_moe_wsel_b_none_p_kernel(
         nc.vector.memset(w2s[:].bitcast(I32), 0)
         nc.gpsimd.memset(w2s_all[:].bitcast(I32), 0)
         nc.gpsimd.memset(gate_rows[:], 0.0)
-        nc.gpsimd.dma_start(gate_rows[0 : G * HALVES, :], gate[:, 0, :].rearrange("r (h c) -> r h c", h=HALVES))
         make_identity(nc, ident[:])
 
         nc.sync.dma_start(w1s_all[STAGE:P, :].bitcast(I32), w1_scales.rearrange("s b m -> (s b) m").bitcast(I32))
         nc.sync.dma_start(list1[:], offs)
         nc.sync.dma_start(xw[0][:], x_words[ORDER[0]].rearrange("p t d -> p (t d)").bitcast(I32))
+        first_words = w1_words[ORDER[0]].rearrange("p m d -> p (m d)").bitcast(I32)
+        nc.sync.dma_start(w1w_all[0][:, 0 : E * H // 2], first_words[:, 0 : E * H // 2])
+        nc.sync.dma_start(list2[:], offs2)
+        nc.sync.dma_start(w2s_all[32:96:4, :].bitcast(I32), w2_scales[0].bitcast(I32))
         for q in range(QUADS):
             nc.sync.dma_start(
                 xs[32 * q : 32 * q + 4 * PASSES, :].bitcast(I32),
                 x_scales[:, 4 * q : 4 * q + 4, :].bitcast(I32),
             )
-        nc.sync.dma_start(w1w_all[0][:], w1_words[ORDER[0]].rearrange("p m d -> p (m d)").bitcast(I32))
-        nc.sync.dma_start(list2[:], offs2)
-        nc.sync.dma_start(w2s_all[32:96:4, :].bitcast(I32), w2_scales[0].bitcast(I32))
+        nc.sync.dma_start(w1w_all[0][:, E * H // 2 : E * H], first_words[:, E * H // 2 : E * H])
+        nc.sync.dma_start(gate_rows[0 : G * HALVES, :], gate[:, 0, :].rearrange("r (h c) -> r h c", h=HALVES))
         gather(w1s_picked[:, 0:H], w1s_all[:], list1, 0, H)
         gather(w1s_picked[:, H : G * H], w1s_all[:], list1, H, (G - 1) * H)
-        gather(w2s_picked[:], w2s_all[:], list2, 0, G * N)
+        w2s_picked = [keep.tile([P, 2 * N], U8, name="w2s_picked0", align_bytes=64)]
+        gather(w2s_picked[0][:], w2s_all[:], list2, 0, 2 * N)
         second_words = w1_words[ORDER[1]].rearrange("p m d -> p (m d)").bitcast(I32)
 
         def move_w1_scales(s, j, cols):
@@ -104,8 +106,6 @@ def tile_moe_wsel_b_none_p_kernel(
         for j in range(2, 4):
             move_w1_scales(1, j, slice(0, G * H))
         nc.sync.dma_start(w2w_all[:], w2_words[0].rearrange("p m d -> p (m d)").bitcast(I32))
-        for j in range(4):
-            nc.sync.dma_start(w2s[j:P:32, :].bitcast(I32), w2s_picked[32 + 4 * j : 96 : 16, :].bitcast(I32))
 
         gate_t = psum.tile([P, H], F32, name="gate_t", tag="bank%d" % (G * HALVES - 1))
         nc.tensor.transpose(gate_t[:, 0:P], gate_rows[:], ident[:])
@@ -129,7 +129,16 @@ def tile_moe_wsel_b_none_p_kernel(
             gather(picked[:].bitcast(U32), w1w_all[s][:].bitcast(U32), list1, r * H, count * H)
             return picked
 
-        picked_first = [gather_w1(0, r, 2) for r in range(0, G, 2)]
+        lead, rest = gather_w1(0, 0, 1), gather_w1(0, 1, G - 1)
+        picked_first = [lead[:]] + [rest[:, r * H : (r + 1) * H] for r in range(G - 1)]
+        w2s_picked.append(keep.tile([P, 2 * N], U8, name="w2s_picked1", tag="w1w_all0", align_bytes=64))
+        gather(w2s_picked[1][:], w2s_all[:], list2, 2 * N, 2 * N)
+        for pair in range(2):
+            for j in range(4):
+                nc.sync.dma_start(
+                    w2s[j:P:32, pair * 2 * N : (pair + 1) * 2 * N].bitcast(I32),
+                    w2s_picked[pair][32 + 4 * j : 96 : 16, :].bitcast(I32),
+                )
 
         h_sum = {}
         for r in range(G):
@@ -150,7 +159,7 @@ def tile_moe_wsel_b_none_p_kernel(
                 )
 
         for r in range(G):
-            first_product(0, r, picked_first[r // 2][:, r % 2 * H : (r % 2 + 1) * H])
+            first_product(0, r, picked_first[r])
 
         def turned(r):
             return h_sum[r, 0][:].rearrange("p (h u t) -> p h u t", h=HALVES, u=2)

@@ -18,11 +18,16 @@ MULT = mybir.AluOpType.mult
 
 P = 128
 PASSES = K // 512
-QUADS = 4
 HALVES = T // P
 STAGE = P - 16 * PASSES
-ORDER = (1, 0)
-CUT = 9 * E * H // 16
+W1_ROW = (4, 8)
+W2_ROW = 12
+GATE_ROW = P - G * HALVES
+DIRECT = 0
+TURNED = (1, 2, 3)
+ORDER = (1, 0, 2, 3)
+CUT = 5 * E * H // 8
+EARLY_MOVES = 2
 
 
 def tile_moe_wsel_b_none_p_kernel(
@@ -31,148 +36,161 @@ def tile_moe_wsel_b_none_p_kernel(
     nc = tc.nc
     with ExitStack() as ctx:
         keep = ctx.enter_context(tc.tile_pool(name="keep", bufs=1))
-        work = ctx.enter_context(tc.tile_pool(name="work", bufs=2))
+        reuse = ctx.enter_context(tc.tile_pool(name="reuse", bufs=1))
         psum = ctx.enter_context(tc.psum_pool(name="psum", bufs=1))
 
-        list1 = keep.tile([P, G * H // 16], U16, name="list1")
-        list2 = keep.tile([P, G * N // 16], U16, name="list2")
-        w1s_all = keep.tile([P, E * H], U8, name="w1s_all", align_bytes=64)
-        w2s_all = keep.tile([P, E * N], U8, name="w2s_all", align_bytes=64)
-        w1w_all = [keep.tile([P, E * H], I32, name="w1w_all%d" % s, align_bytes=64) for s in range(PASSES)]
-        w2w_all = keep.tile([P, E * N], I32, name="w2w_all", align_bytes=64)
-        xw = [keep.tile([P, T], I32, name="xw%d" % s, align_bytes=64) for s in range(PASSES)]
-        xs = keep.tile([P, T], U8, name="xs", align_bytes=64)
-        w1s_picked = keep.tile([P, G * H], U8, name="w1s_picked", align_bytes=64)
-        w1s = [keep.tile([P, G * H], U8, name="w1s%d" % s, align_bytes=64) for s in range(PASSES)]
-        lead_scales = keep.tile([P, H], U8, name="lead_scales", align_bytes=64)
-        w2s = keep.tile([P, G * N], U8, name="w2s", align_bytes=64)
-        gate_rows = keep.tile([P, P], F32, name="gate_rows")
-        gate_cols = keep.tile([P, G * HALVES], F32, name="gate_cols")
-        ident = keep.tile([P, P], F32, name="ident")
+        def sbuf(name, cols, dtype):
+            return keep.tile([P, cols], dtype, name=name, align_bytes=64)
+
+        def bank(name, index):
+            return psum.tile([P, H], F32, name=name, tag="bank%d" % index)
+
+        def words_of(packed):
+            return packed.rearrange("p m d -> p (m d)").bitcast(I32)
 
         def gather(dst, window, offsets, first, count):
             nc.vector.tensor_copy(dst, window.indirect(offsets[:, first // 16 : (first + count) // 16]))
 
+        list1 = keep.tile([P, G * H // 16], U16, name="list1")
+        list2 = keep.tile([P, G * N // 16], U16, name="list2")
+        w1s_all = sbuf("w1s_all", E * H, U8)
+        w2s_all = sbuf("w2s_all", E * N, U8)
+        w1w_first = sbuf("w1w_first", E * H, I32)
+        xw_lead = sbuf("xw_lead", P, I32)
+        xs = sbuf("xs", PASSES * T, U8)
+        w1s = [sbuf("w1s%d" % s, G * H, U8) for s in range(PASSES)]
+        w2s = sbuf("w2s", G * N, U8)
+        gate_rows = sbuf("gate_rows", P, F32)
+        gate_cols = sbuf("gate_cols", G * HALVES, F32)
+        gate_full = sbuf("gate_full", T, F32)
+        ident = sbuf("ident", P, F32)
+
         nc.vector.memset(xs[:].bitcast(I32), 0)
+        nc.vector.memset(w2s_all[:].bitcast(I32), 0)
         nc.vector.memset(w1s_all[0:STAGE, :].bitcast(I32), 0)
-        nc.vector.memset(lead_scales[:].bitcast(I32), 0)
-        nc.vector.memset(w1s[0][:, H : G * H].bitcast(I32), 0)
-        nc.vector.memset(w1s[1][:].bitcast(I32), 0)
-        nc.vector.memset(w2s[:].bitcast(I32), 0)
-        nc.gpsimd.memset(w2s_all[:].bitcast(I32), 0)
-        nc.gpsimd.memset(gate_rows[:], 0.0)
+        for plane in w1s + [w2s]:
+            nc.vector.memset(plane[:].bitcast(I32), 0)
+        nc.gpsimd.memset(gate_rows[0:STAGE, :], 0.0)
+        nc.gpsimd.memset(gate_rows[STAGE:GATE_ROW, :], 0.0)
         make_identity(nc, ident[:])
 
+        first_words, second_words = words_of(w1_words[0]), words_of(w1_words[1])
         nc.sync.dma_start(w1s_all[STAGE:P, :].bitcast(I32), w1_scales.rearrange("s b m -> (s b) m").bitcast(I32))
         nc.sync.dma_start(list1[:], offs)
-        nc.sync.dma_start(xw[0][:], x_words[ORDER[0]].rearrange("p t d -> p (t d)").bitcast(I32))
-        first_words = w1_words[ORDER[0]].rearrange("p m d -> p (m d)").bitcast(I32)
-        nc.sync.dma_start(w1w_all[0][:, 0 : E * H // 2], first_words[:, 0 : E * H // 2])
+        nc.sync.dma_start(xw_lead[:], words_of(x_words[0])[:, 0:P])
+        nc.sync.dma_start(gate_rows[GATE_ROW:P, :], gate[:, 0, :].rearrange("r (h c) -> r h c", h=HALVES))
+        nc.sync.dma_start(w1w_first[:, 0 : E * H // 2], first_words[:, 0 : E * H // 2])
         nc.sync.dma_start(list2[:], offs2)
         nc.sync.dma_start(w2s_all[32:96:4, :].bitcast(I32), w2_scales[0].bitcast(I32))
-        for q in range(QUADS):
+        for j in range(4):
             nc.sync.dma_start(
-                xs[32 * q : 32 * q + 4 * PASSES, :].bitcast(I32),
-                x_scales[:, 4 * q : 4 * q + 4, :].bitcast(I32),
+                xs[j:P:32, :].bitcast(I32).rearrange("q (s t) -> q s t", s=PASSES),
+                x_scales[:, j:16:4, :].bitcast(I32).rearrange("s q t -> q s t"),
             )
-        nc.sync.dma_start(w1w_all[0][:, E * H // 2 : E * H], first_words[:, E * H // 2 : E * H])
-        nc.sync.dma_start(gate_rows[0 : G * HALVES, :], gate[:, 0, :].rearrange("r (h c) -> r h c", h=HALVES))
+        nc.sync.dma_start(w1w_first[:, E * H // 2 : E * H], first_words[:, E * H // 2 : E * H])
+
+        w1s_picked = reuse.tile([P, G * H], U8, name="w1s_picked", align_bytes=64, offset=4 * E * N - 64)
+        w1s_laid = sbuf("w1s_laid", G * H, U8)
         gather(w1s_picked[:, 0:H], w1s_all[:], list1, 0, H)
         gather(w1s_picked[:, H : G * H], w1s_all[:], list1, H, (G - 1) * H)
-        w2s_picked = [keep.tile([P, 2 * N], U8, name="w2s_picked0", align_bytes=64)]
-        gather(w2s_picked[0][:], w2s_all[:], list2, 0, 2 * N)
-        second_words = w1_words[ORDER[1]].rearrange("p m d -> p (m d)").bitcast(I32)
+        nc.vector.tensor_copy(w1s_laid[:, 0:H].rearrange("p (j m) -> p m j", j=4), w1s_picked[:, 0:H])
+        nc.vector.tensor_copy(w1s_laid[:, H : G * H].bitcast(I32), w1s_picked[:, H : G * H].bitcast(I32))
+        w2s_picked = sbuf("w2s_picked", G * N, U8)
+        gather(w2s_picked[:], w2s_all[:], list2, 0, G * N)
 
-        def move_w1_scales(s, j, cols):
-            first = STAGE + 16 * ORDER[s] + j
+        def move_w1_scales(s, j):
+            first = STAGE + 16 * s + j
             nc.sync.dma_start(
-                w1s[s][4 * ORDER[s] + j : P : 32, cols].bitcast(I32),
-                w1s_picked[first : first + 13 : 4, cols].bitcast(I32),
+                w1s[s][W1_ROW[s] + j : P : 32, :].bitcast(I32), w1s_laid[first : first + 13 : 4, :].bitcast(I32)
             )
 
-        for q in (0, 2, 1, 3):
-            first, row = STAGE + 16 * ORDER[0] + 4 * q, 32 * q + 4 * ORDER[0]
-            nc.sync.dma_start(
-                lead_scales[row : row + 4, :].bitcast(I32),
-                w1s_picked[first : first + 4, 0:H].bitcast(I32),
-            )
-        nc.sync.dma_start(w1w_all[1][:, 0:CUT], second_words[:, 0:CUT])
+        w2w_all = reuse.tile([P, E * N], I32, name="w2w_all", align_bytes=64, offset=0)
+        xw_rest = reuse.tile([P, P], I32, name="xw_rest", align_bytes=64, offset=4 * E * N)
+        xw_second = reuse.tile([P, T], I32, name="xw_second", align_bytes=64, offset=4 * (E * N + P))
+        w1w_second = reuse.tile([P, E * H], I32, name="w1w_second", align_bytes=64, offset=4 * (E * N + P + T))
         for j in range(4):
-            move_w1_scales(0, j, slice(H, G * H))
-            if j < 2:
-                move_w1_scales(1, j, slice(0, G * H))
-        nc.sync.dma_start(w1w_all[1][:, CUT : E * H], second_words[:, CUT : E * H])
-        nc.sync.dma_start(xw[1][:], x_words[ORDER[1]].rearrange("p t d -> p (t d)").bitcast(I32))
-        for j in range(2, 4):
-            move_w1_scales(1, j, slice(0, G * H))
-        nc.sync.dma_start(w2w_all[:], w2_words[0].rearrange("p m d -> p (m d)").bitcast(I32))
+            move_w1_scales(0, j)
+            if j < EARLY_MOVES:
+                move_w1_scales(1, j)
+        nc.sync.dma_start(w1w_second[:, 0:CUT], second_words[:, 0:CUT])
+        nc.sync.dma_start(xw_rest[:], words_of(x_words[0])[:, P:T])
+        nc.sync.dma_start(w1w_second[:, CUT : E * H], second_words[:, CUT : E * H])
+        nc.sync.dma_start(xw_second[:], words_of(x_words[1]))
+        for j in range(EARLY_MOVES, 4):
+            move_w1_scales(1, j)
+        nc.sync.dma_start(w2w_all[:], words_of(w2_words[0]))
+        for j in range(4):
+            nc.sync.dma_start(
+                w2s[W2_ROW + j : P : 32, :].bitcast(I32), w2s_picked[32 + 4 * j : 96 : 16, :].bitcast(I32)
+            )
+        xw = {(0, 0): xw_lead[:], (0, 1): xw_rest[:], (1, 0): xw_second[:, 0:P], (1, 1): xw_second[:, P:T]}
 
-        gate_t = psum.tile([P, H], F32, name="gate_t", tag="bank%d" % (G * HALVES - 1))
+        gate_t = bank("gate_t", 2 * G - 1)
         nc.tensor.transpose(gate_t[:, 0:P], gate_rows[:], ident[:])
-        nc.scalar.activation(gate_cols[:], gate_t[:, 0 : G * HALVES], COPY)
+        nc.scalar.activation(gate_cols[:], gate_t[:, GATE_ROW:P], COPY)
+        gate_b = bank("gate_b", 2 * G - 3)
+        for half in range(HALVES):
+            col = DIRECT * HALVES + half
+            nc.tensor.transpose(
+                gate_b[:, half * P : (half + 1) * P], gate_cols[:, col : col + 1].to_broadcast([P, P]), ident[:]
+            )
+        nc.scalar.activation(gate_full[:], gate_b[:, 0:T], COPY)
 
-        def warm_up(bank, words):
-            idle = psum.tile([P, H], F32, name="idle", tag="bank%d" % bank)
-            for i in range(2):
-                nc.tensor.matmul_mx(
-                    out=idle[:],
-                    lhsT=xw[0][:, 0:P].bitcast(FP8X4),
-                    lhsT_scale=xs[4 * ORDER[0] : P, 0:P],
-                    rhs=words[:, 0:H].bitcast(FP8X4),
-                    rhs_scale=lead_scales[4 * ORDER[0] : P, :],
-                    start=(i == 0),
-                    stop=(i == 1),
-                )
-
-        def gather_w1(s, r, count):
-            picked = keep.tile([P, count * H], I32, name="w1w_%d_%d" % (s, r), align_bytes=64)
-            gather(picked[:].bitcast(U32), w1w_all[s][:].bitcast(U32), list1, r * H, count * H)
+        def gather_w1(s, window, r):
+            picked = sbuf("w1w_%d_%d" % (s, r), H, U32)
+            dst = picked[:].rearrange("p (j m) -> p m j", j=4) if r == DIRECT else picked[:]
+            gather(dst, window[:].bitcast(U32), list1, r * H, H)
             return picked
 
-        lead, rest = gather_w1(0, 0, 1), gather_w1(0, 1, G - 1)
-        picked_first = [lead[:]] + [rest[:, r * H : (r + 1) * H] for r in range(G - 1)]
-        w2s_picked.append(keep.tile([P, 2 * N], U8, name="w2s_picked1", tag="w1w_all0", align_bytes=64))
-        gather(w2s_picked[1][:], w2s_all[:], list2, 2 * N, 2 * N)
-        for pair in range(2):
-            for j in range(4):
-                nc.sync.dma_start(
-                    w2s[j:P:32, pair * 2 * N : (pair + 1) * 2 * N].bitcast(I32),
-                    w2s_picked[pair][32 + 4 * j : 96 : 16, :].bitcast(I32),
-                )
+        h_sum = {(r, half): bank("h_sum", r * HALVES + half) for r in range(G) for half in range(HALVES)}
 
-        h_sum = {}
-        for r in range(G):
-            for half in range(HALVES):
-                h_sum[r, half] = psum.tile([P, H], F32, name="h_sum", tag="bank%d" % (r * HALVES + half))
-
-        def first_product(s, r, picked):
-            for half in range(HALVES):
-                tok = slice(half * P, (half + 1) * P)
+        def first_product(s, r, half, picked):
+            tokens = xw[s, half].bitcast(FP8X4)
+            token_scales = xs[:, s * T + half * P : s * T + (half + 1) * P]
+            if r == DIRECT:
+                for j in range(4):
+                    nc.tensor.matmul_mx(
+                        out=h_sum[r, half][:, j * P : (j + 1) * P],
+                        lhsT=picked[:, j * P : (j + 1) * P].bitcast(FP8X4),
+                        lhsT_scale=w1s[s][W1_ROW[s] : P, r * H + j * P : r * H + (j + 1) * P],
+                        rhs=tokens,
+                        rhs_scale=token_scales,
+                        start=(s == 0 and j == 0),
+                        stop=(s == PASSES - 1 and j == 3),
+                    )
+            else:
                 nc.tensor.matmul_mx(
                     out=h_sum[r, half][:],
-                    lhsT=xw[s][:, tok].bitcast(FP8X4),
-                    lhsT_scale=xs[4 * ORDER[s] : P, tok],
-                    rhs=picked.bitcast(FP8X4),
-                    rhs_scale=(lead_scales if (s, r) == (0, 0) else w1s[s])[4 * ORDER[s] : P, r * H : (r + 1) * H],
+                    lhsT=tokens,
+                    lhsT_scale=token_scales,
+                    rhs=picked[:].bitcast(FP8X4),
+                    rhs_scale=w1s[s][W1_ROW[s] : P, r * H : (r + 1) * H],
                     start=(s == 0),
                     stop=(s == PASSES - 1),
                 )
 
-        for r in range(G):
-            first_product(0, r, picked_first[r])
+        picked_first = {r: gather_w1(0, w1w_first, r) for r in ORDER}
+        for half in range(HALVES):
+            for r in ORDER:
+                first_product(0, r, half, picked_first[r])
+        for r in ORDER:
+            picked = gather_w1(1, w1w_second, r)
+            for half in range(HALVES):
+                first_product(1, r, half, picked)
 
         def turned(r):
             return h_sum[r, 0][:].rearrange("p (h u t) -> p h u t", h=HALVES, u=2)
 
         def gated_copy(r, half):
             col = r * HALVES + half
-            h_tok = work.tile([P, H], BF16, name="h_tok", bufs=G * HALVES, align_bytes=64)
+            scale = gate_cols[:, col : col + 1]
+            h_tok = sbuf("h_tok%d" % col, H, BF16)
             dst = h_tok[:].rearrange("t (u p e) -> t u p e", u=2, e=2)
             src = h_sum[r, half][:].rearrange("t (p u e) -> t u p e", u=2, e=2)
-            if half == 1 and r > 0:
-                nc.vector.tensor_scalar(dst, src, gate_cols[:, col : col + 1], None, MULT)
-            else:
-                nc.scalar.activation(dst, src, COPY, scale=gate_cols[:, col : col + 1])
+            shared = P // 2 if col == G * HALVES - 1 else 0
+            if shared:
+                nc.vector.tensor_scalar(dst[:, :, 0:shared, :], src[:, :, 0:shared, :], scale, None, MULT)
+            nc.scalar.activation(dst[:, :, shared:P, :], src[:, :, shared:P, :], COPY, scale=scale)
             return h_tok
 
         def turn(r, half, h_tok):
@@ -181,21 +199,32 @@ def tile_moe_wsel_b_none_p_kernel(
                 nc.tensor.transpose(turned(r)[:, half, u, :], words[:, u * P : (u + 1) * P], ident[:])
 
         def turned_copy(r, halves):
-            h_in = work.tile([P, 4 * P * len(halves)], BF16, name="h_in", bufs=G + 1, align_bytes=64)
+            h_in = sbuf("h_in%d_%d" % (r, halves[0]), 4 * P * len(halves), BF16)
             nc.scalar.copy(
                 h_in[:].bitcast(F32).rearrange("p (h t u) -> p h t u", h=len(halves), u=2),
                 turned(r)[:, halves[0] : halves[-1] + 1].rearrange("p h u t -> p h t u"),
             )
             return h_in
 
+        def direct_copy():
+            h_in = sbuf("h_direct", 4 * T, BF16)
+            for half in range(HALVES):
+                nc.vector.tensor_tensor(
+                    h_in[:, half * 4 * P : (half + 1) * 4 * P].rearrange("p (t j) -> p t j", j=4),
+                    h_sum[DIRECT, half][:].rearrange("p (j t) -> p t j", j=4),
+                    gate_full[:, half * P : (half + 1) * P].unsqueeze(2).to_broadcast([P, P, 4]),
+                    MULT,
+                )
+            return h_in
+
         def gather_w2(r):
-            w2w = keep.tile([P, N], I32, name="w2w_%d" % r, align_bytes=64)
-            gather(w2w[:].bitcast(U32), w2w_all[:].bitcast(U32), list2, r * N, N)
+            w2w = sbuf("w2w_%d" % r, N, U32)
+            gather(w2w[:], w2w_all[:].bitcast(U32), list2, r * N, N)
             return w2w
 
-        def quantise(h_in, halves):
-            h_codes = work.tile([P, P * len(halves)], U32, name="h_codes", bufs=G + 1, align_bytes=64)
-            h_scales = work.tile([P, P * len(halves)], U8, name="h_scales", bufs=G + 1, align_bytes=64)
+        def quantise(r, halves, h_in):
+            h_codes = sbuf("h_codes%d_%d" % (r, halves[0]), P * len(halves), U32)
+            h_scales = sbuf("h_scales%d_%d" % (r, halves[0]), P * len(halves), U8)
             nc.vector.quantize_mx(out=h_codes[:].bitcast(FP8X4), scales=h_scales[:], in_=h_in[:])
             return h_codes, h_scales
 
@@ -203,34 +232,28 @@ def tile_moe_wsel_b_none_p_kernel(
             for i, half in enumerate(halves):
                 tok = slice(i * P, (i + 1) * P)
                 for b in range(N // P):
-                    cols = slice(r * N + b * P, r * N + (b + 1) * P)
                     nc.tensor.matmul_mx(
                         out=acc[half, b][:, 0:P],
                         lhsT=w2w[:, b * P : (b + 1) * P].bitcast(FP8X4),
-                        lhsT_scale=w2s[:, cols],
+                        lhsT_scale=w2s[W2_ROW:P, r * N + b * P : r * N + (b + 1) * P],
                         rhs=h_codes[:, tok].bitcast(FP8X4),
                         rhs_scale=h_scales[:, tok],
-                        start=(r == 0),
-                        stop=(r == G - 1),
+                        start=(r == DIRECT),
+                        stop=(r == TURNED[-1]),
                     )
 
-        for r in range(G):
-            first_product(1, r, gather_w1(1, r, 1)[:])
-        h_toks = {(r, half): gated_copy(r, half) for r in range(G) for half in range(HALVES)}
-        for r in range(G):
+        h_direct = direct_copy()
+        h_toks = {(r, half): gated_copy(r, half) for r in TURNED for half in range(HALVES)}
+        for r in TURNED:
             for half in range(HALVES):
                 turn(r, half, h_toks[r, half])
-            if r == G - 2:
-                warm_up(G * HALVES - 1, picked_first[0])
-        pieces = [(r, (0, 1)) for r in range(G - 1)] + [(G - 1, (0,)), (G - 1, (1,))]
-        h_ins = [turned_copy(r, halves) for r, halves in pieces]
-        acc = {}
-        for half in range(HALVES):
-            for b in range(N // P):
-                acc[half, b] = psum.tile([P, H], F32, name="acc", tag="bank%d" % (2 * (2 * half + b) + 1))
+        pieces = [(r, (0, 1)) for r in TURNED[:-1]] + [(TURNED[-1], (0,)), (TURNED[-1], (1,))]
+        h_ins = [h_direct] + [turned_copy(r, halves) for r, halves in pieces]
+        free_banks = (3, 0, 1, 5)
+        acc = {(half, b): bank("acc", free_banks[2 * half + b]) for half in range(HALVES) for b in range(N // P)}
         w2w = [gather_w2(r) for r in range(G)]
-        for (r, halves), h_in in zip(pieces, h_ins):
-            second_product(r, halves, w2w[r], *quantise(h_in, halves))
+        for (r, halves), h_in in zip([(DIRECT, (0, 1))] + pieces, h_ins):
+            second_product(r, halves, w2w[r], *quantise(r, halves, h_in))
 
         for half in range(HALVES):
             res = keep.tile([P, N // P, P], F32, name="res%d" % half)

@@ -23,9 +23,6 @@ STAGE = P - 16 * PASSES
 W1_ROW = (4, 8)
 W2_ROW = 12
 GATE_ROW = P - G * HALVES
-DIRECT = 0
-TURNED = (1, 2, 3)
-ORDER = (1, 0, 2, 3)
 CUT = 5 * E * H // 8
 EARLY_MOVES = 2
 
@@ -53,7 +50,7 @@ def tile_moe_wsel_b_none_p_kernel(
 
         list1 = keep.tile([P, G * H // 16], U16, name="list1")
         list2 = keep.tile([P, G * N // 16], U16, name="list2")
-        w1s_all = sbuf("w1s_all", E * H, U8)
+        w1s_all = reuse.tile([P, E * H], U8, name="w1s_all", align_bytes=64, offset=4 * E * N - 64)
         w2s_all = sbuf("w2s_all", E * N, U8)
         w1w_first = sbuf("w1w_first", E * H, I32)
         xw_lead = sbuf("xw_lead", P, I32)
@@ -62,7 +59,6 @@ def tile_moe_wsel_b_none_p_kernel(
         w2s = sbuf("w2s", G * N, U8)
         gate_rows = sbuf("gate_rows", P, F32)
         gate_cols = sbuf("gate_cols", G * HALVES, F32)
-        gate_full = sbuf("gate_full", T, F32)
         ident = sbuf("ident", P, F32)
 
         nc.vector.memset(xs[:].bitcast(I32), 0)
@@ -89,19 +85,15 @@ def tile_moe_wsel_b_none_p_kernel(
             )
         nc.sync.dma_start(w1w_first[:, E * H // 2 : E * H], first_words[:, E * H // 2 : E * H])
 
-        w1s_picked = reuse.tile([P, G * H], U8, name="w1s_picked", align_bytes=64, offset=4 * E * N - 64)
-        w1s_laid = sbuf("w1s_laid", G * H, U8)
-        gather(w1s_picked[:, 0:H], w1s_all[:], list1, 0, H)
-        gather(w1s_picked[:, H : G * H], w1s_all[:], list1, H, (G - 1) * H)
-        nc.vector.tensor_copy(w1s_laid[:, 0:H].rearrange("p (j m) -> p m j", j=4), w1s_picked[:, 0:H])
-        nc.vector.tensor_copy(w1s_laid[:, H : G * H].bitcast(I32), w1s_picked[:, H : G * H].bitcast(I32))
+        w1s_picked = sbuf("w1s_picked", G * H, U8)
+        gather(w1s_picked[:], w1s_all[:], list1, 0, G * H)
         w2s_picked = sbuf("w2s_picked", G * N, U8)
         gather(w2s_picked[:], w2s_all[:], list2, 0, G * N)
 
         def move_w1_scales(s, j):
             first = STAGE + 16 * s + j
             nc.sync.dma_start(
-                w1s[s][W1_ROW[s] + j : P : 32, :].bitcast(I32), w1s_laid[first : first + 13 : 4, :].bitcast(I32)
+                w1s[s][W1_ROW[s] + j : P : 32, :].bitcast(I32), w1s_picked[first : first + 13 : 4, :].bitcast(I32)
             )
 
         w2w_all = reuse.tile([P, E * N], I32, name="w2w_all", align_bytes=64, offset=0)
@@ -128,52 +120,43 @@ def tile_moe_wsel_b_none_p_kernel(
         gate_t = bank("gate_t", 2 * G - 1)
         nc.tensor.transpose(gate_t[:, 0:P], gate_rows[:], ident[:])
         nc.scalar.activation(gate_cols[:], gate_t[:, GATE_ROW:P], COPY)
-        gate_b = bank("gate_b", 2 * G - 3)
-        for half in range(HALVES):
-            col = DIRECT * HALVES + half
-            nc.tensor.transpose(
-                gate_b[:, half * P : (half + 1) * P], gate_cols[:, col : col + 1].to_broadcast([P, P]), ident[:]
-            )
-        nc.scalar.activation(gate_full[:], gate_b[:, 0:T], COPY)
 
         def gather_w1(s, window, r):
             picked = sbuf("w1w_%d_%d" % (s, r), H, U32)
-            dst = picked[:].rearrange("p (j m) -> p m j", j=4) if r == DIRECT else picked[:]
-            gather(dst, window[:].bitcast(U32), list1, r * H, H)
+            gather(picked[:], window[:].bitcast(U32), list1, r * H, H)
             return picked
 
         h_sum = {(r, half): bank("h_sum", r * HALVES + half) for r in range(G) for half in range(HALVES)}
 
         def first_product(s, r, half, picked):
-            tokens = xw[s, half].bitcast(FP8X4)
-            token_scales = xs[:, s * T + half * P : s * T + (half + 1) * P]
-            if r == DIRECT:
-                for j in range(4):
-                    nc.tensor.matmul_mx(
-                        out=h_sum[r, half][:, j * P : (j + 1) * P],
-                        lhsT=picked[:, j * P : (j + 1) * P].bitcast(FP8X4),
-                        lhsT_scale=w1s[s][W1_ROW[s] : P, r * H + j * P : r * H + (j + 1) * P],
-                        rhs=tokens,
-                        rhs_scale=token_scales,
-                        start=(s == 0 and j == 0),
-                        stop=(s == PASSES - 1 and j == 3),
-                    )
-            else:
+            nc.tensor.matmul_mx(
+                out=h_sum[r, half][:],
+                lhsT=xw[s, half].bitcast(FP8X4),
+                lhsT_scale=xs[:, s * T + half * P : s * T + (half + 1) * P],
+                rhs=picked[:].bitcast(FP8X4),
+                rhs_scale=w1s[s][W1_ROW[s] : P, r * H : (r + 1) * H],
+                start=(s == 0),
+                stop=(s == PASSES - 1),
+            )
+
+        def warm_up(index, words):
+            idle = bank("idle", index)
+            for i in range(2):
                 nc.tensor.matmul_mx(
-                    out=h_sum[r, half][:],
-                    lhsT=tokens,
-                    lhsT_scale=token_scales,
-                    rhs=picked[:].bitcast(FP8X4),
-                    rhs_scale=w1s[s][W1_ROW[s] : P, r * H : (r + 1) * H],
-                    start=(s == 0),
-                    stop=(s == PASSES - 1),
+                    out=idle[:],
+                    lhsT=xw[0, 0].bitcast(FP8X4),
+                    lhsT_scale=xs[:, 0:P],
+                    rhs=words[:].bitcast(FP8X4),
+                    rhs_scale=w1s[0][W1_ROW[0] : P, 0:H],
+                    start=(i == 0),
+                    stop=(i == 1),
                 )
 
-        picked_first = {r: gather_w1(0, w1w_first, r) for r in ORDER}
+        picked_first = [gather_w1(0, w1w_first, r) for r in range(G)]
         for half in range(HALVES):
-            for r in ORDER:
+            for r in range(G):
                 first_product(0, r, half, picked_first[r])
-        for r in ORDER:
+        for r in range(G):
             picked = gather_w1(1, w1w_second, r)
             for half in range(HALVES):
                 first_product(1, r, half, picked)
@@ -187,10 +170,10 @@ def tile_moe_wsel_b_none_p_kernel(
             h_tok = sbuf("h_tok%d" % col, H, BF16)
             dst = h_tok[:].rearrange("t (u p e) -> t u p e", u=2, e=2)
             src = h_sum[r, half][:].rearrange("t (p u e) -> t u p e", u=2, e=2)
-            shared = P // 2 if col == G * HALVES - 1 else 0
-            if shared:
-                nc.vector.tensor_scalar(dst[:, :, 0:shared, :], src[:, :, 0:shared, :], scale, None, MULT)
-            nc.scalar.activation(dst[:, :, shared:P, :], src[:, :, shared:P, :], COPY, scale=scale)
+            if half == 1 and r > 0:
+                nc.vector.tensor_scalar(dst, src, scale, None, MULT)
+            else:
+                nc.scalar.activation(dst, src, COPY, scale=scale)
             return h_tok
 
         def turn(r, half, h_tok):
@@ -204,17 +187,6 @@ def tile_moe_wsel_b_none_p_kernel(
                 h_in[:].bitcast(F32).rearrange("p (h t u) -> p h t u", h=len(halves), u=2),
                 turned(r)[:, halves[0] : halves[-1] + 1].rearrange("p h u t -> p h t u"),
             )
-            return h_in
-
-        def direct_copy():
-            h_in = sbuf("h_direct", 4 * T, BF16)
-            for half in range(HALVES):
-                nc.vector.tensor_tensor(
-                    h_in[:, half * 4 * P : (half + 1) * 4 * P].rearrange("p (t j) -> p t j", j=4),
-                    h_sum[DIRECT, half][:].rearrange("p (j t) -> p t j", j=4),
-                    gate_full[:, half * P : (half + 1) * P].unsqueeze(2).to_broadcast([P, P, 4]),
-                    MULT,
-                )
             return h_in
 
         def gather_w2(r):
@@ -238,21 +210,21 @@ def tile_moe_wsel_b_none_p_kernel(
                         lhsT_scale=w2s[W2_ROW:P, r * N + b * P : r * N + (b + 1) * P],
                         rhs=h_codes[:, tok].bitcast(FP8X4),
                         rhs_scale=h_scales[:, tok],
-                        start=(r == DIRECT),
-                        stop=(r == TURNED[-1]),
+                        start=(r == 0),
+                        stop=(r == G - 1),
                     )
 
-        h_direct = direct_copy()
-        h_toks = {(r, half): gated_copy(r, half) for r in TURNED for half in range(HALVES)}
-        for r in TURNED:
+        h_toks = {(r, half): gated_copy(r, half) for r in range(G) for half in range(HALVES)}
+        for r in range(G):
             for half in range(HALVES):
                 turn(r, half, h_toks[r, half])
-        pieces = [(r, (0, 1)) for r in TURNED[:-1]] + [(TURNED[-1], (0,)), (TURNED[-1], (1,))]
-        h_ins = [h_direct] + [turned_copy(r, halves) for r, halves in pieces]
-        free_banks = (3, 0, 1, 5)
-        acc = {(half, b): bank("acc", free_banks[2 * half + b]) for half in range(HALVES) for b in range(N // P)}
+            if r == G - 2:
+                warm_up(G * HALVES - 1, picked_first[0])
+        pieces = [(r, (0, 1)) for r in range(G - 1)] + [(G - 1, (0,)), (G - 1, (1,))]
+        h_ins = [turned_copy(r, halves) for r, halves in pieces]
+        acc = {(half, b): bank("acc", 2 * (2 * half + b) + 1) for half in range(HALVES) for b in range(N // P)}
         w2w = [gather_w2(r) for r in range(G)]
-        for (r, halves), h_in in zip([(DIRECT, (0, 1))] + pieces, h_ins):
+        for (r, halves), h_in in zip(pieces, h_ins):
             second_product(r, halves, w2w[r], *quantise(r, halves, h_in))
 
         for half in range(HALVES):

@@ -25,6 +25,7 @@ W2_ROW = 12
 GATE_ROW = P - G * HALVES
 CUT = 5 * E * H // 8
 EARLY_MOVES = 2
+WHOLE = 1
 
 
 def tile_moe_wsel_b_none_p_kernel(
@@ -189,11 +190,6 @@ def tile_moe_wsel_b_none_p_kernel(
             )
             return h_in
 
-        def gather_w2(r):
-            w2w = sbuf("w2w_%d" % r, N, U32)
-            gather(w2w[:], w2w_all[:].bitcast(U32), list2, r * N, N)
-            return w2w
-
         def quantise(r, halves, h_in):
             h_codes = sbuf("h_codes%d_%d" % (r, halves[0]), P * len(halves), U32)
             h_scales = sbuf("h_scales%d_%d" % (r, halves[0]), P * len(halves), U8)
@@ -206,7 +202,7 @@ def tile_moe_wsel_b_none_p_kernel(
                 for b in range(N // P):
                     nc.tensor.matmul_mx(
                         out=acc[half, b][:, 0:P],
-                        lhsT=w2w[:, b * P : (b + 1) * P].bitcast(FP8X4),
+                        lhsT=w2w[:, r * N + b * P : r * N + (b + 1) * P].bitcast(FP8X4),
                         lhsT_scale=w2s[W2_ROW:P, r * N + b * P : r * N + (b + 1) * P],
                         rhs=h_codes[:, tok].bitcast(FP8X4),
                         rhs_scale=h_scales[:, tok],
@@ -220,16 +216,20 @@ def tile_moe_wsel_b_none_p_kernel(
                 turn(r, half, h_toks[r, half])
             if r == G - 2:
                 warm_up(G * HALVES - 1, picked_first[0])
-        pieces = [(r, (0, 1)) for r in range(G - 1)] + [(G - 1, (0,)), (G - 1, (1,))]
+        pieces = [(r, (0, 1)) for r in range(WHOLE)] + [(r, (half,)) for half in range(HALVES) for r in range(WHOLE, G)]
         h_ins = [turned_copy(r, halves) for r, halves in pieces]
         acc = {(half, b): bank("acc", 2 * (2 * half + b) + 1) for half in range(HALVES) for b in range(N // P)}
-        w2w = [gather_w2(r) for r in range(G)]
+        w2w = sbuf("w2w", G * N, U32)
+        gather(w2w[:], w2w_all[:].bitcast(U32), list2, 0, G * N)
         for (r, halves), h_in in zip(pieces, h_ins):
-            second_product(r, halves, w2w[r], *quantise(r, halves, h_in))
+            second_product(r, halves, w2w, *quantise(r, halves, h_in))
 
         for half in range(HALVES):
             res = keep.tile([P, N // P, P], F32, name="res%d" % half)
-            nc.vector.tensor_copy(res[:, 0, :], acc[half, 0][:, 0:P])
+            if half == 0:
+                nc.scalar.copy(res[:, 0, :], acc[half, 0][:, 0:P])
+            else:
+                nc.vector.tensor_copy(res[:, 0, :], acc[half, 0][:, 0:P])
             nc.scalar.copy(res[:, 1, :], acc[half, 1][:, 0:P])
             (nc.sync if half == 0 else nc.scalar).dma_start(
                 out.rearrange("(b p) t -> p b t", p=P)[:, :, half * P : (half + 1) * P], res[:]

@@ -231,6 +231,6 @@ def tile_moe_wsel_b_none_p_kernel(
             else:
                 nc.vector.tensor_copy(res[:, 0, :], acc[half, 0][:, 0:P])
             nc.scalar.copy(res[:, 1, :], acc[half, 1][:, 0:P])
-            (nc.sync if half == 0 else nc.scalar).dma_start(
+            nc.sync.dma_start(
                 out.rearrange("(b p) t -> p b t", p=P)[:, :, half * P : (half + 1) * P], res[:]
             )

@@ -71,20 +71,24 @@ def tile_moe_wsel_b_none_p_kernel(
         nc.gpsimd.memset(gate_rows[STAGE:GATE_ROW, :], 0.0)
         make_identity(nc, ident[:])
 
-        first_words, second_words = words_of(w1_words[0]), words_of(w1_words[1])
-        nc.sync.dma_start(w1s_all[STAGE:P, :].bitcast(I32), w1_scales.rearrange("s b m -> (s b) m").bitcast(I32))
-        nc.sync.dma_start(list1[:], offs)
-        nc.sync.dma_start(xw_lead[:], words_of(x_words[0])[:, 0:P])
-        nc.sync.dma_start(gate_rows[GATE_ROW:P, :], gate[:, 0, :].rearrange("r (h c) -> r h c", h=HALVES))
-        nc.sync.dma_start(w1w_first[:, 0 : E * H // 2], first_words[:, 0 : E * H // 2])
-        nc.sync.dma_start(list2[:], offs2)
-        nc.sync.dma_start(w2s_all[32:96:4, :].bitcast(I32), w2_scales[0].bitcast(I32))
-        for j in range(4):
+        def load_token_scales(j):
             nc.sync.dma_start(
                 xs[j:P:32, :].bitcast(I32).rearrange("q (s t) -> q s t", s=PASSES),
                 x_scales[:, j:16:4, :].bitcast(I32).rearrange("s q t -> q s t"),
             )
+
+        first_words, second_words = words_of(w1_words[0]), words_of(w1_words[1])
+        nc.sync.dma_start(w1s_all[STAGE:P, :].bitcast(I32), w1_scales.rearrange("s b m -> (s b) m").bitcast(I32))
+        nc.sync.dma_start(list1[:], offs)
+        nc.sync.dma_start(xw_lead[:], words_of(x_words[0])[:, 0:P])
+        nc.sync.dma_start(w1w_first[:, 0 : E * H // 2], first_words[:, 0 : E * H // 2])
+        nc.sync.dma_start(gate_rows[GATE_ROW:P, :], gate[:, 0, :].rearrange("r (h c) -> r h c", h=HALVES))
+        nc.sync.dma_start(list2[:], offs2)
+        nc.sync.dma_start(w2s_all[32:96:4, :].bitcast(I32), w2_scales[0].bitcast(I32))
+        for j in range(3):
+            load_token_scales(j)
         nc.sync.dma_start(w1w_first[:, E * H // 2 : E * H], first_words[:, E * H // 2 : E * H])
+        load_token_scales(3)
 
         w1s_picked = sbuf("w1s_picked", G * H, U8)
         gather(w1s_picked[:], w1s_all[:], list1, 0, G * H)
@@ -103,9 +107,11 @@ def tile_moe_wsel_b_none_p_kernel(
         w1w_second = reuse.tile([P, E * H], I32, name="w1w_second", align_bytes=64, offset=4 * (E * N + P + T))
         for j in range(4):
             move_w1_scales(0, j)
-            if j < EARLY_MOVES:
+            if j == 0:
                 move_w1_scales(1, j)
         nc.sync.dma_start(w1w_second[:, 0:CUT], second_words[:, 0:CUT])
+        for j in range(1, EARLY_MOVES):
+            move_w1_scales(1, j)
         nc.sync.dma_start(xw_rest[:], words_of(x_words[0])[:, P:T])
         nc.sync.dma_start(w1w_second[:, CUT : E * H], second_words[:, CUT : E * H])
         nc.sync.dma_start(xw_second[:], words_of(x_words[1]))
@@ -183,7 +189,9 @@ def tile_moe_wsel_b_none_p_kernel(
                 nc.tensor.transpose(turned(r)[:, half, u, :], words[:, u * P : (u + 1) * P], ident[:])
 
         def turned_copy(r, halves):
-            h_in = sbuf("h_in%d_%d" % (r, halves[0]), 4 * P * len(halves), BF16)
+            name = "h_in%d_%d" % (r, halves[0])
+            tag = "last_input" if (r, halves) == pieces[-1] else name
+            h_in = keep.tile([P, 4 * P * len(halves)], BF16, name=name, tag=tag, align_bytes=64)
             nc.scalar.copy(
                 h_in[:].bitcast(F32).rearrange("p (h t u) -> p h t u", h=len(halves), u=2),
                 turned(r)[:, halves[0] : halves[-1] + 1].rearrange("p h u t -> p h t u"),
@@ -225,12 +233,13 @@ def tile_moe_wsel_b_none_p_kernel(
             second_product(r, halves, w2w, *quantise(r, halves, h_in))
 
         for half in range(HALVES):
-            res = keep.tile([P, N // P, P], F32, name="res%d" % half)
-            if half == 0:
-                nc.scalar.copy(res[:, 0, :], acc[half, 0][:, 0:P])
-            else:
-                nc.vector.tensor_copy(res[:, 0, :], acc[half, 0][:, 0:P])
+            tag = "last_input" if half == 0 else "res"
+            res = keep.tile([P, N // P, P], F32, name="res%d" % half, tag=tag, align_bytes=64)
+            nc.vector.tensor_copy(res[:, 0, :], acc[half, 0][:, 0:P])
             nc.scalar.copy(res[:, 1, :], acc[half, 1][:, 0:P])
-            nc.sync.dma_start(
-                out.rearrange("(b p) t -> p b t", p=P)[:, :, half * P : (half + 1) * P], res[:]
-            )
+            rows = out.rearrange("(b p) t -> p b t", p=P)[:, :, half * P : (half + 1) * P]
+            if half == 0:
+                nc.sync.dma_start(rows, res[:])
+            else:
+                for b in range(N // P):
+                    nc.sync.dma_start(rows[:, b, :], res[:, b, :])

from contextlib import ExitStack

import concourse.mybir as mybir
from concourse.masks import make_identity

K, T, E, G, H, N = 1024, 256, 8, 4, 512, 256
FLOPS = 2 * G * T * H * (K + N)

F32 = mybir.dt.float32
BF16 = mybir.dt.bfloat16
I32 = mybir.dt.int32
U32 = mybir.dt.uint32
U16 = mybir.dt.uint16
U8 = mybir.dt.uint8
FP8X4 = mybir.dt.float8_e4m3fn_x4
COPY = mybir.ActivationFunctionType.Copy
MULT = mybir.AluOpType.mult

P = 128
PASSES = K // 512
HALVES = T // P
STAGE = P - 16 * PASSES
W1_ROW = (4, 8)
W2_ROW = 12
GATE_ROW = P - G * HALVES
CUT = 5 * E * H // 8
EARLY_MOVES = 2
WHOLE = 1


def tile_moe_wsel_b_none_p_kernel(
    tc, x_words, x_scales, w1_words, w1_scales, w2_words, w2_scales, gate, offs, offs2, out
):
    nc = tc.nc
    with ExitStack() as ctx:
        keep = ctx.enter_context(tc.tile_pool(name="keep", bufs=1))
        reuse = ctx.enter_context(tc.tile_pool(name="reuse", bufs=1))
        psum = ctx.enter_context(tc.psum_pool(name="psum", bufs=1))

        def sbuf(name, cols, dtype):
            return keep.tile([P, cols], dtype, name=name, align_bytes=64)

        def bank(name, index):
            return psum.tile([P, H], F32, name=name, tag="bank%d" % index)

        def words_of(packed):
            return packed.rearrange("p m d -> p (m d)").bitcast(I32)

        def gather(dst, window, offsets, first, count):
            nc.vector.tensor_copy(dst, window.indirect(offsets[:, first // 16 : (first + count) // 16]))

        list1 = keep.tile([P, G * H // 16], U16, name="list1")
        list2 = keep.tile([P, G * N // 16], U16, name="list2")
        w1s_all = reuse.tile([P, E * H], U8, name="w1s_all", align_bytes=64, offset=4 * E * N - 64)
        w2s_all = sbuf("w2s_all", E * N, U8)
        w1w_first = sbuf("w1w_first", E * H, I32)
        xw_lead = sbuf("xw_lead", P, I32)
        xs = sbuf("xs", PASSES * T, U8)
        w1s = [sbuf("w1s%d" % s, G * H, U8) for s in range(PASSES)]
        w2s = sbuf("w2s", G * N, U8)
        gate_rows = sbuf("gate_rows", P, F32)
        gate_cols = sbuf("gate_cols", G * HALVES, F32)
        ident = sbuf("ident", P, F32)

        nc.vector.memset(xs[:].bitcast(I32), 0)
        nc.vector.memset(w2s_all[:].bitcast(I32), 0)
        nc.vector.memset(w1s_all[0:STAGE, :].bitcast(I32), 0)
        for plane in w1s + [w2s]:
            nc.vector.memset(plane[:].bitcast(I32), 0)
        nc.gpsimd.memset(gate_rows[0:STAGE, :], 0.0)
        nc.gpsimd.memset(gate_rows[STAGE:GATE_ROW, :], 0.0)
        make_identity(nc, ident[:])

        def load_token_scales(j):
            nc.sync.dma_start(
                xs[j:P:32, :].bitcast(I32).rearrange("q (s t) -> q s t", s=PASSES),
                x_scales[:, j:16:4, :].bitcast(I32).rearrange("s q t -> q s t"),
            )

        first_words, second_words = words_of(w1_words[0]), words_of(w1_words[1])
        nc.sync.dma_start(w1s_all[STAGE:P, :].bitcast(I32), w1_scales.rearrange("s b m -> (s b) m").bitcast(I32))
        nc.sync.dma_start(list1[:], offs)
        nc.sync.dma_start(xw_lead[:], words_of(x_words[0])[:, 0:P])
        nc.sync.dma_start(w1w_first[:, 0 : E * H // 2], first_words[:, 0 : E * H // 2])
        nc.sync.dma_start(gate_rows[GATE_ROW:P, :], gate[:, 0, :].rearrange("r (h c) -> r h c", h=HALVES))
        nc.sync.dma_start(list2[:], offs2)
        nc.sync.dma_start(w2s_all[32:96:4, :].bitcast(I32), w2_scales[0].bitcast(I32))
        for j in range(3):
            load_token_scales(j)
        nc.sync.dma_start(w1w_first[:, E * H // 2 : E * H], first_words[:, E * H // 2 : E * H])
        load_token_scales(3)

        w1s_picked = sbuf("w1s_picked", G * H, U8)
        gather(w1s_picked[:], w1s_all[:], list1, 0, G * H)
        w2s_picked = sbuf("w2s_picked", G * N, U8)
        gather(w2s_picked[:], w2s_all[:], list2, 0, G * N)

        def move_w1_scales(s, j):
            first = STAGE + 16 * s + j
            nc.sync.dma_start(
                w1s[s][W1_ROW[s] + j : P : 32, :].bitcast(I32), w1s_picked[first : first + 13 : 4, :].bitcast(I32)
            )

        w2w_all = reuse.tile([P, E * N], I32, name="w2w_all", align_bytes=64, offset=0)
        xw_rest = reuse.tile([P, P], I32, name="xw_rest", align_bytes=64, offset=4 * E * N)
        xw_second = reuse.tile([P, T], I32, name="xw_second", align_bytes=64, offset=4 * (E * N + P))
        w1w_second = reuse.tile([P, E * H], I32, name="w1w_second", align_bytes=64, offset=4 * (E * N + P + T))
        for j in range(4):
            move_w1_scales(0, j)
            if j == 0:
                move_w1_scales(1, j)
        nc.sync.dma_start(w1w_second[:, 0:CUT], second_words[:, 0:CUT])
        for j in range(1, EARLY_MOVES):
            move_w1_scales(1, j)
        nc.sync.dma_start(xw_rest[:], words_of(x_words[0])[:, P:T])
        nc.sync.dma_start(w1w_second[:, CUT : E * H], second_words[:, CUT : E * H])
        nc.sync.dma_start(xw_second[:], words_of(x_words[1]))
        for j in range(EARLY_MOVES, 4):
            move_w1_scales(1, j)
        nc.sync.dma_start(w2w_all[:], words_of(w2_words[0]))
        for j in range(4):
            nc.sync.dma_start(
                w2s[W2_ROW + j : P : 32, :].bitcast(I32), w2s_picked[32 + 4 * j : 96 : 16, :].bitcast(I32)
            )
        xw = {(0, 0): xw_lead[:], (0, 1): xw_rest[:], (1, 0): xw_second[:, 0:P], (1, 1): xw_second[:, P:T]}

        gate_t = bank("gate_t", 2 * G - 1)
        nc.tensor.transpose(gate_t[:, 0:P], gate_rows[:], ident[:])
        nc.scalar.activation(gate_cols[:], gate_t[:, GATE_ROW:P], COPY)

        def gather_w1(s, window, r):
            picked = sbuf("w1w_%d_%d" % (s, r), H, U32)
            gather(picked[:], window[:].bitcast(U32), list1, r * H, H)
            return picked

        h_sum = {(r, half): bank("h_sum", r * HALVES + half) for r in range(G) for half in range(HALVES)}

        def first_product(s, r, half, picked):
            nc.tensor.matmul_mx(
                out=h_sum[r, half][:],
                lhsT=xw[s, half].bitcast(FP8X4),
                lhsT_scale=xs[:, s * T + half * P : s * T + (half + 1) * P],
                rhs=picked[:].bitcast(FP8X4),
                rhs_scale=w1s[s][W1_ROW[s] : P, r * H : (r + 1) * H],
                start=(s == 0),
                stop=(s == PASSES - 1),
            )

        def warm_up(index, words):
            idle = bank("idle", index)
            for i in range(2):
                nc.tensor.matmul_mx(
                    out=idle[:],
                    lhsT=xw[0, 0].bitcast(FP8X4),
                    lhsT_scale=xs[:, 0:P],
                    rhs=words[:].bitcast(FP8X4),
                    rhs_scale=w1s[0][W1_ROW[0] : P, 0:H],
                    start=(i == 0),
                    stop=(i == 1),
                )

        picked_first = [gather_w1(0, w1w_first, r) for r in range(G)]
        for half in range(HALVES):
            for r in range(G):
                first_product(0, r, half, picked_first[r])
        for r in range(G):
            picked = gather_w1(1, w1w_second, r)
            for half in range(HALVES):
                first_product(1, r, half, picked)

        def turned(r):
            return h_sum[r, 0][:].rearrange("p (h u t) -> p h u t", h=HALVES, u=2)

        def gated_copy(r, half):
            col = r * HALVES + half
            scale = gate_cols[:, col : col + 1]
            h_tok = sbuf("h_tok%d" % col, H, BF16)
            dst = h_tok[:].rearrange("t (u p e) -> t u p e", u=2, e=2)
            src = h_sum[r, half][:].rearrange("t (p u e) -> t u p e", u=2, e=2)
            if half == 1 and r > 0:
                nc.vector.tensor_scalar(dst, src, scale, None, MULT)
            else:
                nc.scalar.activation(dst, src, COPY, scale=scale)
            return h_tok

        def turn(r, half, h_tok):
            words = h_tok[:].bitcast(F32)
            for u in range(2):
                nc.tensor.transpose(turned(r)[:, half, u, :], words[:, u * P : (u + 1) * P], ident[:])

        def turned_copy(r, halves):
            name = "h_in%d_%d" % (r, halves[0])
            tag = "last_input" if (r, halves) == pieces[-1] else name
            h_in = keep.tile([P, 4 * P * len(halves)], BF16, name=name, tag=tag, align_bytes=64)
            nc.scalar.copy(
                h_in[:].bitcast(F32).rearrange("p (h t u) -> p h t u", h=len(halves), u=2),
                turned(r)[:, halves[0] : halves[-1] + 1].rearrange("p h u t -> p h t u"),
            )
            return h_in

        def quantise(r, halves, h_in):
            h_codes = sbuf("h_codes%d_%d" % (r, halves[0]), P * len(halves), U32)
            h_scales = sbuf("h_scales%d_%d" % (r, halves[0]), P * len(halves), U8)
            nc.vector.quantize_mx(out=h_codes[:].bitcast(FP8X4), scales=h_scales[:], in_=h_in[:])
            return h_codes, h_scales

        def second_product(r, halves, w2w, h_codes, h_scales):
            for i, half in enumerate(halves):
                tok = slice(i * P, (i + 1) * P)
                for b in range(N // P):
                    nc.tensor.matmul_mx(
                        out=acc[half, b][:, 0:P],
                        lhsT=w2w[:, r * N + b * P : r * N + (b + 1) * P].bitcast(FP8X4),
                        lhsT_scale=w2s[W2_ROW:P, r * N + b * P : r * N + (b + 1) * P],
                        rhs=h_codes[:, tok].bitcast(FP8X4),
                        rhs_scale=h_scales[:, tok],
                        start=(r == 0),
                        stop=(r == G - 1),
                    )

        h_toks = {(r, half): gated_copy(r, half) for r in range(G) for half in range(HALVES)}
        for r in range(G):
            for half in range(HALVES):
                turn(r, half, h_toks[r, half])
            if r == G - 2:
                warm_up(G * HALVES - 1, picked_first[0])
        pieces = [(r, (0, 1)) for r in range(WHOLE)] + [(r, (half,)) for half in range(HALVES) for r in range(WHOLE, G)]
        h_ins = [turned_copy(r, halves) for r, halves in pieces]
        acc = {(half, b): bank("acc", 2 * (2 * half + b) + 1) for half in range(HALVES) for b in range(N // P)}
        w2w = sbuf("w2w", G * N, U32)
        gather(w2w[:], w2w_all[:].bitcast(U32), list2, 0, G * N)
        for (r, halves), h_in in zip(pieces, h_ins):
            second_product(r, halves, w2w, *quantise(r, halves, h_in))

        for half in range(HALVES):
            tag = "last_input" if half == 0 else "res"
            res = keep.tile([P, N // P, P], F32, name="res%d" % half, tag=tag, align_bytes=64)
            nc.vector.tensor_copy(res[:, 0, :], acc[half, 0][:, 0:P])
            nc.scalar.copy(res[:, 1, :], acc[half, 1][:, 0:P])
            rows = out.rearrange("(b p) t -> p b t", p=P)[:, :, half * P : (half + 1) * P]
            if half == 0:
                nc.sync.dma_start(rows, res[:])
            else:
                for b in range(N // P):
                    nc.sync.dma_start(rows[:, b, :], res[:, b, :])
